import numpy as np, ml_dtypes
CORES = [36,164,52,180,100,228,116,244]
N = 8
BF = ml_dtypes.bfloat16
M, D, LV, CAP = 1024, 4, 4, 192
P, H = N * M, 2 ** LV - 1
def ancestors(t):
    p, s = t >> 1, t & 1
    L = np.full((8, P + 1), P, np.int64); R = L.copy()
    for k in range(LV):
        a = np.where(s == 1, p, np.take_along_axis(L, p, 1)); b = np.where(s == 0, p, np.take_along_axis(R, p, 1))
        L[:, :P] = a; R[:, :P] = b
    return L[:, :P], R[:, :P]
def wants(t):
    L, R = ancestors(t); w = np.zeros((8, N, P + 1), bool); g = np.arange(8)[:, None]; r = (np.arange(P) // M)[None]
    w[g, r, L] = True; w[g, r, R] = True
    return w[:, :, :P].reshape(8, N, N, M)
def fit(rng, t):
    w = wants(t); L, R = ancestors(t)
    for g, r, q in np.argwhere(np.count_nonzero(w, axis=3) > CAP):
        if r != q:
            c = rng.permutation(np.flatnonzero(w[g, r, q]))[CAP:] + q * M; a = r * M
            x = t[g, a:a + M]; x[np.isin(L[g, a:a + M], c) | np.isin(R[g, a:a + M], c)] = 2 * P
def grid(rng):
    lev = np.array([c.bit_length() - 1 for c in range(1, H + 1)]); k = rng.random((H,) * D); s = np.zeros((H,) * D, np.int64)
    for d in range(D):
        e = lev.reshape([H if i == d else 1 for i in range(D)]); s = s + e; k = k + (0.75 + 0.5 * rng.random()) * e
    for d in range(D):
        u = np.moveaxis(k, d, 0)
        for c in range(2, H + 1): u[c - 1] = np.maximum(u[c - 1], u[c // 2 - 1])
    o = np.lexsort((s.reshape(-1), k.reshape(-1)))[:P]; o = o[rng.permutation(P)]
    num = np.full(H ** D, P); num[o] = np.arange(P); c = np.stack(np.unravel_index(o, (H,) * D)) + 1
    t = np.full((D, P), 2 * P)
    for d in range(D):
        b = c.copy(); b[d] = np.maximum(b[d] // 2, 1)
        t[d] = np.where(c[d] > 1, 2 * num[np.ravel_multi_index(tuple(b - 1), (H,) * D)] + c[d] % 2, 2 * P)
    return t
def vals(rng):
    return (rng.standard_normal((N, 128, M), dtype=np.float32) * np.exp2(rng.integers(-2, 3, (N, 128, 1)))).astype(np.float32)
def made(rng, v, t):
    for d in range(D): fit(rng, t[:, d])
    return {"v": v, "tree": np.repeat(t.reshape(1, 8, D * P).astype(np.int32), N, axis=0)}
def heaps(o):
    b = o[:len(o) // H * H].reshape(-1, H); c = np.arange(2, H + 1)
    return b[:, 1:], 2 * b[:, c // 2 - 1] + c % 2
def setup_inputs(rng):
    return made(rng, vals(rng), np.stack([grid(rng) for g in range(8)]))
def setup_inputs_full(rng):
    t = np.full((8, D, P), 2 * P); n3 = min(CAP, M - 2 * CAP); n4 = max(0, min(CAP, M - 3 * CAP))
    for g, d in np.ndindex(8, D):
        o = np.stack([q * M + rng.permutation(M) for q in range(N)]); a = np.roll(o, -(1 + (g + d) % (N - 1)), axis=0)
        s = rng.integers(0, 2, (3, N, CAP)); x = t[g, d]
        x[o[:, CAP:2 * CAP]] = 2 * a[:, :CAP] + s[0]
        x[o[:, 2 * CAP:2 * CAP + n3]] = 2 * o[:, CAP:CAP + n3] + s[1][:, :n3]
        x[o[:, 3 * CAP:3 * CAP + n4]] = 2 * o[:, 2 * CAP:2 * CAP + n4] + s[2][:, :n4]
    return made(rng, vals(rng), t)
def setup_inputs_chains(rng):
    t = np.full((8, D, P), 2 * P); k = P // LV
    for g, d in np.ndindex(8, D):
        o = np.concatenate([[0, P - 1], 1 + rng.permutation(P - 2)])[:k * LV].reshape(k, LV)
        s = rng.integers(0, 2, (k, LV)); s[0] = 1; s[0, 1] = 0; s[1] = 0; s[1, 1] = 1
        x = t[g, d]; x[o[:, 1:]] = 2 * o[:, :-1] + s[:, 1:]
    return made(rng, vals(rng), t)
def setup_inputs_near(rng):
    t = np.full((8, D, P), 2 * P)
    for g, d in np.ndindex(8, D):
        x = t[g, d]
        if (g + d) % 3 == 1:
            for q in range(N):
                i, e = heaps(q * M + rng.permutation(M)); x[i] = e
        if (g + d) % 3 == 2:
            i, e = heaps(rng.permutation(P)); x[i] = e
    return made(rng, vals(rng), t)
def setup_inputs_spread(rng):
    d = setup_inputs(rng); k = (N, 1, M)
    d["v"] = (d["v"] * np.exp2(rng.integers(-6, 7, k)) * (rng.random(k) > 0.0625)).astype(np.float32); return d
def check_inputs(d):
    bad = []; a = np.abs(d["v"].astype(np.float64)); tr = d["tree"].astype(np.int64)
    if not ((a == 0) | ((a >= 2.0 ** -60) & (a <= 2.0 ** 60))).all(): bad.append("sizes")
    if (tr != tr[:1]).any(): bad.append("alike")
    if tr.min() < 0 or tr.max() > 2 * P: return bad + ["codes"]
    other = ~np.eye(N, dtype=bool)
    for k in range(D):
        t = tr[0][:, k * P:(k + 1) * P]
        for g in range(8):
            c = t[g][t[g] < 2 * P]; up = np.append(t[g] >> 1, P); x = np.arange(P)
            if len(np.unique(c)) < len(c): bad.append("sides")
            for i in range(LV): x = up[x]
            if (x != P).any(): bad.append("levels")
        if (np.count_nonzero(wants(t), axis=3)[:, other] > CAP).any(): bad.append("wanted")
    return sorted(set(bad))
def reference(v, tree):
    u = np.zeros((8, 16, P + 1), np.float32)
    u[:, :, :P] = v.reshape(N, 8, 16, M).transpose(1, 2, 0, 3).reshape(8, 16, P)
    for d in range(D):
        L, R = ancestors(tree[0][:, d * P:(d + 1) * P].astype(np.int64))
        for g in range(8):
            s = u[g][:, L[g]] + u[g][:, R[g]]
            u[g, :, :P] = u[g, :, :P] - np.float32(0.5) * s
    y = u[:, :, :P].reshape(8, 16, N, M).transpose(2, 0, 1, 3).reshape(N, 128, M)
    return {"y": np.ascontiguousarray(y)}

@@ -1,0 +1,448 @@
+from concourse.bass import DstId, RemoteDMATransfer
+from concourse.mybir import AluOpType, ActivationFunctionType
+
+N, M, D = 8, 1024, 4
+P = N * M
+BLK = M // N
+BIG, CC, CLAMP = 262144.0, 16384.0, 98304.0
+KEEP = 65536 + 8191
+CFG = {"ways": [["PDDHDDD", "PDDHDDD", "PPDHHDD", "PPDHHDD"], ["PPDHDDD", "PPDHDDD", "PPDHHDD", "PPDHHDD"],
+                ["PDDHHDD", "PDDHHDD", "PPDHHDD", "PPDHHDD"], ["PPDHHHD", "PPDHHHD", "PPDHHHD", "PPDHHHD"]],
+       "lots": [[0], [1], [2, 3]], "slope": 20.0, "seed": 146, "noise": 0.5, "heng": "VSG"}
+
+SCRATCH = {
+    "xt": ("sbuf", [128, 256], "int32"),
+    "xf": ("sbuf", [128, M], "int32"),
+    "hf": ("sbuf", [128, M], "bfloat16"),
+    "ht": ("sbuf", [128, M], "bfloat16"),
+    "tb": ("sbuf", [128, P + 16], "bfloat16"),
+    "r0": ("sbuf", [128, M], "bfloat16"),
+    "rr": ("sbuf", [128, 2 * D * M], "bfloat16"),
+    "ones": ("sbuf", [128, M], "bfloat16"),
+    "sel": ("sbuf", [128, M], "bfloat16"),
+    "wt": ("sbuf", [128, 144], "float32"),
+    "ee": ("sbuf", [128, 144], "float32"),
+    "e2": ("sbuf", [128, 72], "float32"),
+    "zz": ("sbuf", [128, 12 * 144], "bfloat16"),
+    "onef": ("sbuf", [128, 256], "float32"),
+    "rot": ("sbuf", [128, 256], "float32"),
+    "i64": ("sbuf", [128, 64], "int32"),
+    "jj": ("sbuf", [128, 4], "int32"),
+    "kc": ("sbuf", [128, 4], "float32"),
+    "jc": ("sbuf", [128, 4], "float32"),
+    "l0": ("sbuf", [128, 64], "uint16"),
+    "off": ("sbuf", [128, 2 * D * 64], "uint16"),
+    "xa": ("sbuf", [128, 3 * D * 64], "float32"),
+    "yi": ("sbuf", [128, D * 128], "int32"),
+    "ls": ("sbuf", [128, D * 128], "uint16"),
+    "wa": ("sbuf", [128, P + 8], "float32"),
+    "wb": ("sbuf", [128, P + 8], "float32"),
+    "ga": ("sbuf", [128, M], "float32"),
+    "gs": ("sbuf", [128, M], "float32"),
+    "yo": ("sbuf", [128, M], "float32"),
+    "yf": ("sbuf", [128, M], "float32"),
+    "dsrc": ("dram", [N, 128, BLK], "float32"),
+    "ddst": ("dram", [N, 128, BLK], "float32"),
+    "pw0": ("psum", [128, 512], "float32"),
+    "pw1": ("psum", [128, 512], "float32"),
+    "pr0": ("psum", [128, 512], "float32"),
+    "pr1": ("psum", [128, 512], "float32"),
+    "pr2": ("psum", [128, 512], "float32"),
+    "pr3": ("psum", [128, 512], "float32"),
+    "pc0": ("psum", [128, 512], "float32"),
+    "pc1": ("psum", [128, 512], "float32"),
+}
+SEMAPHORES = ["cV", "cS", "cP", "cG", "tree0", "lay", "ld0", "ld1", "own", "sent", "arr0", "arr1",
+              "rep0", "rep1", "rep2", "rep3", "fa0", "fa1", "fa2", "fa3", "st0", "st1"]
+
+ALU, ACT = AluOpType, ActivationFunctionType
+
+
+def build(g, core, T, topo, rank):
+    ops = []
+    Q = {"V": g.vector, "S": g.scalar, "P": g.tensor, "G": g, "Y": g.sync, "A": g.scalar}
+
+    def node(kind, engs, cost, emit, rd, wr, sem=None, n=0, xfer=0.0, gat=False, by=0, rows=0):
+        ops.append({"kind": kind, "engs": engs, "cost": cost, "emit": emit, "rd": list(rd), "wr": list(wr),
+                    "sem": sem, "n": n, "xfer": xfer, "gat": gat, "by": by, "rows": rows})
+
+    def comp(eng, cost, emit, rd, wr, gat=False):
+        node("c", {eng: cost}, cost, lambda e: emit(), rd, wr, gat=gat)
+
+    def copy(out, in_, n, rd, wr, per=1.0, scale=None, engs="VS"):
+        def emit(e):
+            if e == "G":
+                return [g.affine_select(out, in_, [[0, n]], ALU.is_ge, 0.0, 0, 0)]
+            if e == "V":
+                if scale is None:
+                    return [g.vector.tensor_copy(out, in_)]
+                return [g.vector.tensor_scalar(out, in_, scale, None, ALU.mult)]
+            if scale is None:
+                return [g.scalar.activation(out, in_, ACT.Copy)]
+            return [g.scalar.activation(out, in_, ACT.Copy, scale=scale)]
+        c = {"V": 0.06 + n * per * 1e-3, "S": 0.075 + n * per * 1e-3, "G": 0.2 + n * 2e-3}
+        node("c", {e: c[e] for e in engs}, c["V"], emit, rd, wr, gat=per > 1)
+
+    def ts(out, in0, s1, s2, op0, op1, n, rd, wr):
+        if op1 is None:
+            comp("V", 0.06 + n * 1e-3, lambda: [g.vector.tensor_scalar(out, in0, s1, None, op0)], rd, wr)
+        else:
+            comp("V", 0.06 + n * 1e-3, lambda: [g.vector.tensor_scalar(out, in0, s1, s2, op0, op1)], rd, wr)
+
+    def tt(out, a, b, op, cyc, rd, wr, gat=False):
+        comp("V", 0.06 + cyc * 1e-3, lambda: [g.vector.tensor_tensor(out, a, b, op)], rd, wr, gat=gat)
+
+    def fill(ap, val, cyc, wr):
+        comp("V", 0.06 + cyc * 1e-3, lambda: [g.vector.memset(ap, val)], [], wr)
+
+    def dma(eng, pairs, sem, rd, wr, nbytes, rows):
+        q = Q[eng]
+        e = "S" if eng == "A" else eng
+        node("d", {e: 0.06 * len(pairs)}, 0.06 * len(pairs),
+             lambda _e: [q.dma_start(o, i) for o, i in pairs], rd, list(wr) + [("ring", sem)], sem=sem, n=16 * len(pairs),
+             xfer=nbytes / 400e3 + rows * 0.02 / 16, by=nbytes, rows=rows)
+
+    def remote(items, sem, rd, tok):
+        ne = min(len(topo.engines(core, T.cores[r])) for _s, _d, r in items)
+        w = ne // (1 if len(items) == 1 else 2 if len(items) == 2 else 4)
+
+        def emit(_e):
+            trs = []
+            for k, (src, dst, r) in enumerate(items):
+                mask = sum(1 << x for x in topo.engines(core, T.cores[r])[k * w:(k + 1) * w])
+                rid, pid = topo.addr(T.cores[r], core)
+                trs.append(RemoteDMATransfer(dst_ids=[DstId(rid=rid, pnc=pid)], dma_engine_mask=mask,
+                                             remote_sem=T.sem[sem], src=src, dst=dst))
+            g.remote_dma_fused(trs, local_sem=T.sem.sent)
+            return []
+        node("r", {"G": 0.4}, 0.4, emit, rd, [tok, ("ring", "sent")], sem="sent", n=w * len(items), xfer=128 / w * 0.04,
+             rows=128 / w)
+        return w * len(items)
+
+    def arrive(sem, n, toks, wr):
+        node("x", {}, 0.0, None, toks, wr, sem=sem, n=n)
+
+    W = [T.wa, T.wb]
+
+    def wtok(b, k, blks, halves=(0, 1)):
+        return [("w", b, k, q, h) for q in blks for h in halves]
+
+    def wall(b):
+        return [t for k in range(N) for t in wtok(b, k, range(N))] + [("wz", b)]
+
+    dma("A", [(T.xt[:, :], T.tree[rank:rank + 1, :])], "tree0", [], ["xt"], 131072, 128)
+    mine = rank // 4
+    for s, h in enumerate((1 - mine, mine)):
+        dma("Y", [(T.dsrc[4 * h:4 * h + 4, 16 * j:16 * j + 16, :], T.v[64 * h:64 * h + 64, BLK * j:BLK * j + BLK])
+                  for j in range(N)], "ld%d" % s, [], [("dsrc", h)], 262144, 512)
+
+    fill(T.ones[:, :], 1.0, 512, ["ones"])
+    comp("G", 2.2, lambda: [g.affine_select(T.sel[:, :], T.ones[:, :], [[-1, 8], [0, 8], [-8, 16]], ALU.is_equal, 0.0, 0, 1)],
+         ["ones"], ["sel"])
+    for b, val in enumerate((1024.0, 128.0, 1.0, BIG)):
+        fill(T.wt[:, 36 * b:36 * b + 36], val, 64, [("wt", b)])
+    comp("G", 0.5, lambda: [g.affine_select(T.ee[:, :], T.wt[:, :], [[-4, 4], [-1, 4], [-16, 9]], ALU.is_equal, 0.0, 0, 1)],
+         [("wt", b) for b in range(4)], ["ee"])
+    comp("G", 0.3, lambda: [g.iota(T.i64[:, :], [[16, 64]], 0, 1)], [], ["i64"])
+    fill(T.onef[:, :], 1.0, 256, ["onef"])
+    fill(T.zz[:, :], 0.0, 864, ["z0", "z1", "z2"])
+    fill(T.tb[:, P:P + 16], 64.0, 64, ["tbz"])
+    fill(T.wa[:, P:P + 8], 0.0, 64, [("wz", 0)])
+    fill(T.wb[:, P:P + 8], 0.0, 64, [("wz", 1)])
+    tt(T.e2[:, 0:36], T.ee[:, 0:36], T.ee[:, 36:72], ALU.add, 72, ["ee"], ["e2a"])
+    tt(T.e2[:, 36:72], T.e2[:, 0:36], T.ee[:, 72:108], ALU.add, 72, ["ee", "e2a"], ["e2b"])
+    copy(T.zz[:, 15:576:16], T.e2[:, 36:72], 64, ["e2b"], ["z0"], engs="V")
+    copy(T.zz[:, 576 + 15:1152:16], T.ee[:, 108:144], 64, ["ee"], ["z1"], engs="V")
+    tt(T.zz[:, 1152 + 15:1728:16], T.e2[:, 36:72], T.ee[:, 108:144], ALU.add, 72, ["ee", "e2b"], ["z2"])
+    ts(T.jj[:, 0:1], T.i64[:, 0:1], 4, None, ALU.arith_shift_right, None, 64, ["i64"], ["jj"])
+    ts(T.kc[:, 0:1], T.jj[:, 0:1], -1024.0, 8192.0, ALU.mult, ALU.add, 64, ["jj"], ["kc"])
+    ts(T.jc[:, 0:1], T.jj[:, 0:1], 1008.0, None, ALU.mult, None, 64, ["jj"], ["jc"])
+    ts(T.l0[:, :], T.i64[:, :], T.jc[:, 0:1], None, ALU.add, None, 64, ["i64", "jc"], ["l0"])
+
+    for s, h in enumerate((1 - mine, mine)):
+        peers = [r for r in range(4 * h, 4 * h + 4) if r != rank]
+        got = remote([(T.dsrc[r], T.wa[:, BLK * rank:BLK * rank + BLK], r) for r in peers], "arr%d" % s, [("dsrc", h)], ("s", s))
+        arrive("arr%d" % s, got, [("s", s)], wtok(0, 0, peers))
+    dma("Y", [(T.wa[:, BLK * rank:BLK * rank + BLK], T.dsrc[rank])], "own", [("dsrc", mine)], wtok(0, 0, [rank]), 65536, 128)
+    comp("G", 0.7, lambda: [g.affine_select(T.rot[:, :], T.onef[:, :], [[0, 2], [-1, 128]], ALU.is_equal, 0.0, 0, 1)],
+         ["onef"], ["rot"])
+
+    SH, AND = ALU.logical_shift_right, ALU.bitwise_and
+    for b, (a1, a2, o1, o2) in enumerate(((8, 71, SH, AND), (11, None, SH, None), (1, 127, SH, AND), (1, None, AND, None))):
+        ts(T.xf[:, 256 * b:256 * b + 256], T.xt[:, :], a1, a2, o1, o2, 256, ["xt"], [("xf", b)])
+        copy(T.hf[:, 256 * b:256 * b + 256], T.xf[:, 256 * b:256 * b + 256], 256, [("xf", b)], [("hf", b)])
+        dma("A", [(T.ht[32 * b:32 * b + 32, :], T.hf[:, 256 * b:256 * b + 256])], "lay", [("hf", b)], [("ht", b)], 65536, 128)
+    PR = [T.pr0, T.pr1, T.pr2, T.pr3]
+    nb = [0]
+
+    def bank():
+        nb[0] += 1
+        return (nb[0] - 1) % 4
+
+    for jx in range(N):
+        for qh in range(2):
+            k = bank()
+
+            def mm(jx=jx, qh=qh, k=k):
+                return [g.tensor.matmul(PR[k][:, 128 * a:128 * a + 128], T.sel[:, 128 * (4 * qh + a):128 * (4 * qh + a) + 128],
+                                        T.ht[:, 128 * jx:128 * jx + 128], True, True) for a in range(4)]
+            comp("P", 0.3, mm, ["sel"] + [("ht", b) for b in range(4)], [("pr", k)])
+            c0 = M * jx + 512 * qh
+            copy(T.tb[:, c0:c0 + 512], PR[k][:, :], 512, [], [("pr", k), ("tb", jx, qh)])
+    tball = [("tb", jx, qh) for jx in range(N) for qh in range(2)] + ["tbz"]
+
+    def lookup(out, c0, offs, o0, rd, tok):
+        for h in range(2):
+            copy(out[:, c0 + 512 * h:c0 + 512 * h + 512], T.tb[:, 0:P + 16].indirect(offs[:, o0 + 32 * h:o0 + 32 * h + 32]),
+                 512, tball + rd, [(tok, h)], per=1.6)
+
+    lookup(T.r0, 0, T.l0, 0, ["l0"], "r0")
+    PC = [T.pc0, T.pc1]
+
+    def deal(d, col, parts, rd):
+        def mm():
+            out, last = [], 16 * len(parts) - 1
+            for kind, buf, c0 in parts:
+                z0 = 144 * (4 * kind + d)
+                for i in range(16):
+                    out.append(g.tensor.matmul(PC[d % 2][:, col:col + 64], T.zz[:, z0 + 15 - i:z0 + 143 - i],
+                                               buf[:, c0 + i:c0 + M:16], len(out) == 0, len(out) == last))
+            return out
+        comp("P", 0.55 * len(parts), mm, ["z0", "z1", "z2"] + rd, [("pc", d % 2)])
+
+    def lists(d):
+        pc, bk = PC[d % 2], ("pc", d % 2)
+        o1, o2, c1, c2 = 128 * d, 128 * d + 64, 2 * M * d, 2 * M * d + M
+        r0, r1, r2 = [("r0", 0), ("r0", 1)], [(("r1", d), 0), (("r1", d), 1)], [(("r2", d), 0), (("r2", d), 1)]
+        deal(d, 0, [(0, T.r0, 0)], r0)
+        ts(T.off[:, o1:o1 + 64], pc[:, 0:64], float(P), None, ALU.min, None, 64, [], [bk, ("o1", d)])
+        ts(T.yi[:, o1:o1 + 64], pc[:, 0:64], T.kc[:, 0:1], None, ALU.add, None, 64, ["kc"], [bk, ("y1", d)])
+        lookup(T.rr, c1, T.off, o1, [("o1", d)], ("r1", d))
+        deal(d, 64, [(0, T.rr, c1)], r1)
+        ts(T.off[:, o2:o2 + 64], pc[:, 64:128], float(P), None, ALU.min, None, 64, [], [bk, ("o2", d)])
+        lookup(T.rr, c2, T.off, o2, [("o2", d)], ("r2", d))
+        x = 192 * d
+        deal(d, 128, [(1, T.r0, 0), (2, T.rr, c1)], r0 + r1)
+        comp("S", 0.14, lambda: [g.scalar.activation(T.xa[:, x:x + 64], pc[:, 128:192], ACT.Abs, bias=-BIG)], [], [bk, ("x1", d)])
+        deal(d, 192, [(1, T.r0, 0), (2, T.rr, c2)], r0 + r2)
+        comp("S", 0.14, lambda: [g.scalar.activation(T.xa[:, x + 64:x + 128], pc[:, 192:256], ACT.Abs, bias=CC - BIG)],
+             [], [bk, ("x2", d)])
+        tt(T.xa[:, x + 128:x + 192], T.xa[:, x:x + 64], T.xa[:, x + 64:x + 128], ALU.min, 128, [("x1", d), ("x2", d)], [("x3", d)])
+        ts(T.yi[:, o2:o2 + 64], T.xa[:, x + 128:x + 192], CLAMP, T.kc[:, 0:1], ALU.min, ALU.add, 64, [("x3", d), "kc"], [("y2", d)])
+        ts(T.yi[:, o1:o1 + 128], T.yi[:, o1:o1 + 128], KEEP, None, AND, None, 128, [], [("y1", d), ("y2", d)])
+        ts(T.ls[:, o1:o1 + 128], T.yi[:, o1:o1 + 128], float(P), None, ALU.min, None, 128, [("y1", d), ("y2", d)], [("ls", d)])
+
+    def spread(d):
+        b = d % 2
+        w = W[b]
+        ways = CFG["ways"][d]
+        quarter = (2, 3, 0, 1) if d == 0 and mine == 0 else (0, 1, 2, 3)
+        for lot in CFG["lots"]:
+            pairs, rd, wr, count = [], [], [], 0
+            for k in range(1, N):
+                cs = [quarter[t] for t in lot if ways[t][k - 1] == "D"]
+                if cs:
+                    s, c0, c1 = 16 * k, 256 * cs[0], 256 * cs[-1] + 256
+                    pairs.append((w[0:128 - s, M * k + c0:M * k + c1], w[s:128, c0:c1]))
+                    pairs.append((w[128 - s:128, M * k + c0:M * k + c1], w[0:s, c0:c1]))
+                    rd += wtok(b, 0, range(c0 // BLK, c1 // BLK))
+                    wr += wtok(b, k, range(c0 // BLK, c1 // BLK))
+                    count += len(cs)
+            if pairs:
+                dma("Y", pairs, "rep%d" % d, sorted(set(rd)), wr, 131072 * count, 64 * len(pairs))
+        for t in range(4):
+            blks, c0 = (2 * quarter[t], 2 * quarter[t] + 1), 256 * quarter[t]
+            for k in range(1, N):
+                if ways[t][k - 1] == "P":
+                    p = bank()
+                    comp("P", 0.55, lambda k=k, p=p, c0=c0: [g.tensor.matmul(PR[p][:, 0:256], T.rot[:, 16 * k:16 * k + 128],
+                                                                           w[:, c0:c0 + 256], True, True)],
+                         ["rot"] + wtok(b, 0, blks), [("pr", p)])
+                    copy(w[:, M * k + c0:M * k + c0 + 256], PR[p][:, 0:256], 256, [], [("pr", p)] + wtok(b, k, blks))
+                if ways[t][k - 1] == "H":
+                    for h in range(2):
+                        copy(w[64 * h:64 * h + 64, M * k + c0:M * k + c0 + 256],
+                             w[64 - 64 * h:128 - 64 * h, M * (k - 4) + c0:M * (k - 4) + c0 + 256], 256,
+                             wtok(b, k - 4, blks, (1 - h,)), wtok(b, k, blks, (h,)), engs=CFG["heng"] if d else "VS")
+
+    PW = [T.pw0, T.pw1]
+
+    def step(d, c0, n):
+        b = d % 2
+        blks = range(c0 // BLK, (c0 + n) // BLK)
+        win = W[b][:, 0:P + 8]
+        o1, o2 = 128 * d + c0 // 16, 128 * d + 64 + c0 // 16
+        copy(T.ga[:, c0:c0 + n], win.indirect(T.ls[:, o2:o2 + n // 16]), n, wall(b) + [("ls", d)],
+             [("ga", q) for q in blks], per=1.6, engs="S")
+        tt(T.gs[:, c0:c0 + n], win.indirect(T.ls[:, o1:o1 + n // 16]), T.ga[:, c0:c0 + n], ALU.add, 1.6 * n,
+           wall(b) + [("ls", d)] + [("ga", q) for q in blks], [("gs", q) for q in blks], gat=True)
+        out, wr = (W[1 - b], wtok(1 - b, 0, blks)) if d < D - 1 else (T.yo, [("yo", q) for q in blks])
+        tt(out[:, c0:c0 + n], T.gs[:, c0:c0 + n], PW[c0 // 512][:, c0 % 512:c0 % 512 + n], ALU.subtract, n,
+           [("gs", q) for q in blks], wr + [("pw", c0 // 512)])
+
+    for d in range(D):
+        lists(d)
+    for d in range(D):
+        spread(d)
+        for h in range(2):
+            copy(PW[h][:, :], W[d % 2][:, 512 * h:512 * h + 512], 512, wtok(d % 2, 0, range(4 * h, 4 * h + 4)), [("pw", h)],
+                 scale=2.0)
+        if d < D - 1:
+            for c in range(4):
+                step(d, 256 * c, 256)
+
+    pair = rank // 2
+    turns = [[2 * (pair ^ t), 2 * (pair ^ t) + 1] for t in (1, 2, 3)] + [[rank ^ 1], [rank]]
+    for t, qs in enumerate(turns):
+        c0, n = BLK * qs[0], BLK * len(qs)
+        step(D - 1, c0, n)
+        copy(T.yf[:, c0:c0 + n], T.yo[:, c0:c0 + n], n, [("yo", q) for q in qs], [("yf", q) for q in qs], scale=0.0625, engs="S")
+        if t < 4:
+            got = remote([(T.yf[:, BLK * q:BLK * q + BLK], T.ddst[rank], q) for q in qs], "fa%d" % t,
+                         [("yf", q) for q in qs], ("f", t))
+            arrive("fa%d" % t, got, [("f", t)], [("dd", t)])
+    for t in (4, 0, 1, 2, 3):
+        qs = turns[t]
+        a, z = qs[0], qs[-1] + 1
+        for e, js in (("Y", range(0, 4)), ("A", range(4, 8))):
+            if t < 4:
+                src, rd = [T.ddst[a:z, 16 * j:16 * j + 16, :] for j in js], [("dd", t)]
+            else:
+                src, rd = [T.yf[16 * j:16 * j + 16, BLK * a:BLK * z] for j in js], [("yf", a)]
+            dma(e, [(T.y[16 * a:16 * z, BLK * j:BLK * j + BLK], s) for j, s in zip(js, src)], "st0" if e == "Y" else "st1",
+                rd, [], 32768 * len(qs), 64 * len(qs))
+    return ops, Q
+
+
+def plan(ops):
+    n = len(ops)
+    deps = [set() for _ in range(n)]
+    soft = [set() for _ in range(n)]
+    writer, readers, group = {}, {}, {}
+    for i, o in enumerate(ops):
+        if o["kind"] == "d":
+            group.setdefault(o["sem"], []).append(i)
+    for i, o in enumerate(ops):
+        for t in o["rd"]:
+            if t in writer:
+                deps[i].add(writer[t])
+        for t in o["wr"]:
+            if t in writer:
+                deps[i].add(writer[t])
+            deps[i].update(readers.get(t, ()))
+        for t in o["rd"]:
+            readers.setdefault(t, []).append(i)
+        for t in o["wr"]:
+            writer[t] = i
+            readers[t] = []
+        deps[i].discard(i)
+        soft[i] = {j for j in deps[i] if o["kind"] in "dr" and ops[j]["kind"] == o["kind"] and ops[j]["sem"] == o["sem"]}
+        deps[i] -= soft[i]
+        for j in list(deps[i]):
+            if ops[j]["kind"] == "d":
+                deps[i].update(group[ops[j]["sem"]])
+    tail = {"c": 0.1, "d": 2.0, "r": 2.5, "x": 0.0}
+    succ = [[] for _ in range(n)]
+    for i in range(n):
+        for j in sorted(deps[i] | soft[i]):
+            succ[j].append(i)
+    prio = [0.0] * n
+    todo = [len(s) for s in succ]
+    stack = [i for i in range(n) if todo[i] == 0]
+    while stack:
+        i = stack.pop()
+        prio[i] = ops[i]["cost"] + ops[i]["xfer"] + max(
+            [prio[k] + (0.0 if i in soft[k] else tail[ops[i]["kind"]]) for k in succ[i]] + [tail[ops[i]["kind"]]])
+        for j in deps[i] | soft[i]:
+            todo[j] -= 1
+            if todo[j] == 0:
+                stack.append(j)
+    x = CFG["seed"]
+    for i in range(n):
+        x = (x * 1103515245 + 12345) % 2147483648
+        prio[i] += CFG["noise"] * (x / 2147483648.0)
+    prio[0] += 100.0
+    left = [len(deps[i] | soft[i]) for i in range(n)]
+    ready = [i for i in range(n) if left[i] == 0]
+    free = {e: 0.0 for e in "VSPGY"}
+    rings = [0.0, 0.0]
+    end, order = [0.0] * n, []
+    while ready:
+        cand = []
+        for i in ready:
+            t0 = max([end[j] for j in deps[i]] + [0.0])
+            if ops[i]["kind"] == "x":
+                cand = [(t0, i, None)]
+                break
+            e = min(ops[i]["engs"], key=lambda x: (max(t0, free[x]) + ops[i]["engs"][x], x))
+            cand.append((max(t0, free[e]), i, e))
+        first = min(c[0] for c in cand)
+        t0, i, e = max(cand, key=lambda c: (prio[c[1]] - CFG["slope"] * max(c[0] - first - 0.1, 0.0), -c[1]))
+        o = ops[i]
+        if e is None:
+            end[i] = t0
+        else:
+            free[e] = t0 + o["engs"][e]
+            if o["kind"] == "c":
+                end[i] = free[e] + tail["c"]
+            elif o["kind"] == "d":
+                rings[0] = max(rings[0], t0 + 0.06) + o["xfer"]
+                end[i] = max(rings[0], free[e]) + tail["d"]
+            else:
+                rings[1] = max(rings[1], free[e]) + o["xfer"]
+                rings[0] = max(rings[0], free[e]) + 0.3 * o["xfer"]
+                end[i] = rings[1] + tail["r"]
+        order.append((i, e, t0))
+        ready.remove(i)
+        for k in succ[i]:
+            left[k] -= 1
+            if left[k] == 0:
+                ready.append(k)
+    return order, deps, group, end
+
+
+def rank_program(g, core, T, topo):
+    rank = T.rank_of(core)
+    if rank is None:
+        return
+    ops, Q = build(g, core, T, topo, rank)
+    order, deps, group, _end = plan(ops)
+    total = {s: sum(ops[i]["n"] for i in m) for s, m in group.items()}
+    count = {e: 0 for e in "VSPG"}
+    done, seen, sent = {}, {}, 0
+    for i, e, _t in order:
+        o = ops[i]
+        if o["kind"] == "x":
+            done[i] = (o["sem"], o["n"])
+            total[o["sem"]] = o["n"]
+            continue
+        need = {}
+        for j in deps[i]:
+            s, v = done[j]
+            if s == "cP" and e == "P":
+                continue
+            need[s] = max(need.get(s, 0), v)
+        for s in sorted(need):
+            if need[s] > seen.get((e, s), 0):
+                Q[e].wait_ge(T.sem[s], need[s])
+                seen[(e, s)] = need[s]
+        ins = o["emit"](e)
+        if o["kind"] == "c":
+            for x in ins:
+                x.then_inc(T.sem["c" + e], 1)
+            count[e] += len(ins)
+            done[i] = ("c" + e, count[e])
+        elif o["kind"] == "d":
+            for x in ins:
+                x.then_inc(T.sem[o["sem"]], 16)
+            done[i] = (o["sem"], total[o["sem"]])
+        else:
+            sent += o["n"]
+    for e in "VSPG":
+        total["c" + e] = count[e]
+    total["sent"] = sent
+    for s in sorted(total):
+        if s[:2] != "st" and total[s] > max([v for (_q, x), v in seen.items() if x == s] + [0]):
+            g.wait_ge(T.sem[s], total[s])
+    g.sync.wait_ge(T.sem.st0, total["st0"])
+    g.scalar.wait_ge(T.sem.st1, total["st1"])

@@ -1,66 +1,33 @@
 from concourse.bass import DstId, RemoteDMATransfer
-from concourse.mybir import AluOpType, ActivationFunctionType
+from concourse.mybir import AluOpType as ALU, ActivationFunctionType as ACT
 
 N, M, D = 8, 1024, 4
-P = N * M
-BLK = M // N
-BIG, CC, CLAMP = 262144.0, 16384.0, 98304.0
-KEEP = 65536 + 8191
-CFG = {"ways": [["PDDHDDD", "PDDHDDD", "PPDHHDD", "PPDHHDD"], ["PPDHDDD", "PPDHDDD", "PPDHHDD", "PPDHHDD"],
-                ["PDDHHDD", "PDDHHDD", "PPDHHDD", "PPDHHDD"], ["PPDHHHD", "PPDHHHD", "PPDHHHD", "PPDHHHD"]],
-       "lots": [[0], [1], [2, 3]], "slope": 20.0, "seed": 146, "noise": 0.5, "heng": "VSG"}
+P, BLK = N * M, M // N
+BIG, CC, CLAMP, KEEP = 262144.0, 16384.0, 98304.0, 65536 + 8191
+CFG = {"ways": [["DDDHDDD"] * 4, ["PDDHDDD"] * 4, ["PPDHDDD", "PPDHDDD", "PPDHHDD", "PPDHHDD"], ["PPDHDDD"] * 4],
+       "lots": [[0, 1], [2, 3]], "plots": [[0], [1], [2], [3]], "slope": 20.0, "seed": 0,
+       "noise": 0.0, "heng": ["VSG", "G", "VSG", "VSG"], "trans": False, "rate": 600e3, "row": 0.01, "td": 1.6,
+       "tr": 2.2, "gat": 1.6, "pe": 0.55}
 
-SCRATCH = {
-    "xt": ("sbuf", [128, 256], "int32"),
-    "xf": ("sbuf", [128, M], "int32"),
-    "hf": ("sbuf", [128, M], "bfloat16"),
-    "ht": ("sbuf", [128, M], "bfloat16"),
-    "tb": ("sbuf", [128, P + 16], "bfloat16"),
-    "r0": ("sbuf", [128, M], "bfloat16"),
-    "rr": ("sbuf", [128, 2 * D * M], "bfloat16"),
-    "ones": ("sbuf", [128, M], "bfloat16"),
-    "sel": ("sbuf", [128, M], "bfloat16"),
-    "wt": ("sbuf", [128, 144], "float32"),
-    "ee": ("sbuf", [128, 144], "float32"),
-    "e2": ("sbuf", [128, 72], "float32"),
-    "zz": ("sbuf", [128, 12 * 144], "bfloat16"),
-    "onef": ("sbuf", [128, 256], "float32"),
-    "rot": ("sbuf", [128, 256], "float32"),
-    "i64": ("sbuf", [128, 64], "int32"),
-    "jj": ("sbuf", [128, 4], "int32"),
-    "kc": ("sbuf", [128, 4], "float32"),
-    "jc": ("sbuf", [128, 4], "float32"),
-    "l0": ("sbuf", [128, 64], "uint16"),
-    "off": ("sbuf", [128, 2 * D * 64], "uint16"),
-    "xa": ("sbuf", [128, 3 * D * 64], "float32"),
-    "yi": ("sbuf", [128, D * 128], "int32"),
-    "ls": ("sbuf", [128, D * 128], "uint16"),
-    "wa": ("sbuf", [128, P + 8], "float32"),
-    "wb": ("sbuf", [128, P + 8], "float32"),
-    "ga": ("sbuf", [128, M], "float32"),
-    "gs": ("sbuf", [128, M], "float32"),
-    "yo": ("sbuf", [128, M], "float32"),
-    "yf": ("sbuf", [128, M], "float32"),
-    "dsrc": ("dram", [N, 128, BLK], "float32"),
-    "ddst": ("dram", [N, 128, BLK], "float32"),
-    "pw0": ("psum", [128, 512], "float32"),
-    "pw1": ("psum", [128, 512], "float32"),
-    "pr0": ("psum", [128, 512], "float32"),
-    "pr1": ("psum", [128, 512], "float32"),
-    "pr2": ("psum", [128, 512], "float32"),
-    "pr3": ("psum", [128, 512], "float32"),
-    "pc0": ("psum", [128, 512], "float32"),
-    "pc1": ("psum", [128, 512], "float32"),
-}
-SEMAPHORES = ["cV", "cS", "cP", "cG", "tree0", "lay", "ld0", "ld1", "own", "sent", "arr0", "arr1",
+SCRATCH = {"dsrc": ("dram", [N, 128, BLK], "float32"), "ddst": ("dram", [N, 128, BLK], "float32")}
+for _t, _l in (("int32", (("xt", 256), ("xf", M), ("i64", 4), ("jj", 4), ("yi", D * 128))),
+               ("bfloat16", (("hf", M), ("ht", M), ("tb", P + 16), ("r0", M), ("rr", 2 * D * M), ("ones", M), ("sel", M),
+                             ("zz", 12 * 144))),
+               ("uint16", (("off", D * 128), ("ls", D * 128))),
+               ("float32", (("wt", 144), ("ee", 144), ("e2", 72), ("onef", 256), ("rot", 256), ("kc", 4),
+                            ("xa", 3 * D * 64), ("wa", P + 8), ("wb", P + 8), ("ga", M), ("gs", M), ("yo", M), ("yf", M)))):
+    for _n, _c in _l:
+        SCRATCH[_n] = ("sbuf", [128, _c], _t)
+for _n in ("pw0", "pw1", "pr0", "pr1", "pr2", "pr3", "pc0", "pc1"):
+    SCRATCH[_n] = ("psum", [128, 512], "float32")
+SEMAPHORES = ["cV", "cS", "cP", "cG", "tree0", "lay", "r0", "ld0", "ld1", "own", "sent", "arr0", "arr1",
               "rep0", "rep1", "rep2", "rep3", "fa0", "fa1", "fa2", "fa3", "st0", "st1"]
-
-ALU, ACT = AluOpType, ActivationFunctionType
 
 
 def build(g, core, T, topo, rank):
     ops = []
     Q = {"V": g.vector, "S": g.scalar, "P": g.tensor, "G": g, "Y": g.sync, "A": g.scalar}
+    GAT, PE = CFG["gat"], CFG["pe"]
 
     def node(kind, engs, cost, emit, rd, wr, sem=None, n=0, xfer=0.0, gat=False, by=0, rows=0):
         ops.append({"kind": kind, "engs": engs, "cost": cost, "emit": emit, "rd": list(rd), "wr": list(wr),
@@ -81,13 +48,11 @@ def build(g, core, T, topo, rank):
                 return [g.scalar.activation(out, in_, ACT.Copy)]
             return [g.scalar.activation(out, in_, ACT.Copy, scale=scale)]
         c = {"V": 0.06 + n * per * 1e-3, "S": 0.075 + n * per * 1e-3, "G": 0.2 + n * 2e-3}
-        node("c", {e: c[e] for e in engs}, c["V"], emit, rd, wr, gat=per > 1)
+        node("c", {e: c[e] for e in engs}, c[engs[0]], emit, rd, wr, gat=per > 1)
 
     def ts(out, in0, s1, s2, op0, op1, n, rd, wr):
-        if op1 is None:
-            comp("V", 0.06 + n * 1e-3, lambda: [g.vector.tensor_scalar(out, in0, s1, None, op0)], rd, wr)
-        else:
-            comp("V", 0.06 + n * 1e-3, lambda: [g.vector.tensor_scalar(out, in0, s1, s2, op0, op1)], rd, wr)
+        more = [] if op1 is None else [op1]
+        comp("V", 0.06 + n * 1e-3, lambda: [g.vector.tensor_scalar(out, in0, s1, s2, op0, *more)], rd, wr)
 
     def tt(out, a, b, op, cyc, rd, wr, gat=False):
         comp("V", 0.06 + cyc * 1e-3, lambda: [g.vector.tensor_tensor(out, a, b, op)], rd, wr, gat=gat)
@@ -95,12 +60,13 @@ def build(g, core, T, topo, rank):
     def fill(ap, val, cyc, wr):
         comp("V", 0.06 + cyc * 1e-3, lambda: [g.vector.memset(ap, val)], [], wr)
 
+    def pick(out, in_, pat, cost, rd, wr):
+        comp("G", cost, lambda: [g.affine_select(out, in_, pat, ALU.is_equal, 0.0, 0, 1)], rd, wr)
+
     def dma(eng, pairs, sem, rd, wr, nbytes, rows):
-        q = Q[eng]
-        e = "S" if eng == "A" else eng
-        node("d", {e: 0.06 * len(pairs)}, 0.06 * len(pairs),
-             lambda _e: [q.dma_start(o, i) for o, i in pairs], rd, list(wr) + [("ring", sem)], sem=sem, n=16 * len(pairs),
-             xfer=nbytes / 400e3 + rows * 0.02 / 16, by=nbytes, rows=rows)
+        node("d", {"S" if eng == "A" else eng: 0.06 * len(pairs)}, 0.06 * len(pairs),
+             lambda _e: [Q[eng].dma_start(o, i) for o, i in pairs], rd, list(wr) + [("ring", sem)], sem=sem,
+             n=16 * len(pairs), xfer=nbytes / CFG["rate"] + rows * CFG["row"] / 16, by=nbytes, rows=rows)
 
     def remote(items, sem, rd, tok):
         ne = min(len(topo.engines(core, T.cores[r])) for _s, _d, r in items)
@@ -119,9 +85,6 @@ def build(g, core, T, topo, rank):
              rows=128 / w)
         return w * len(items)
 
-    def arrive(sem, n, toks, wr):
-        node("x", {}, 0.0, None, toks, wr, sem=sem, n=n)
-
     W = [T.wa, T.wb]
 
     def wtok(b, k, blks, halves=(0, 1)):
@@ -137,13 +100,11 @@ def build(g, core, T, topo, rank):
                   for j in range(N)], "ld%d" % s, [], [("dsrc", h)], 262144, 512)
 
     fill(T.ones[:, :], 1.0, 512, ["ones"])
-    comp("G", 2.2, lambda: [g.affine_select(T.sel[:, :], T.ones[:, :], [[-1, 8], [0, 8], [-8, 16]], ALU.is_equal, 0.0, 0, 1)],
-         ["ones"], ["sel"])
+    pick(T.sel[:, :], T.ones[:, :], [[-1, 8], [0, 8], [-8, 16]], 2.2, ["ones"], ["sel"])
     for b, val in enumerate((1024.0, 128.0, 1.0, BIG)):
         fill(T.wt[:, 36 * b:36 * b + 36], val, 64, [("wt", b)])
-    comp("G", 0.5, lambda: [g.affine_select(T.ee[:, :], T.wt[:, :], [[-4, 4], [-1, 4], [-16, 9]], ALU.is_equal, 0.0, 0, 1)],
-         [("wt", b) for b in range(4)], ["ee"])
-    comp("G", 0.3, lambda: [g.iota(T.i64[:, :], [[16, 64]], 0, 1)], [], ["i64"])
+    pick(T.ee[:, :], T.wt[:, :], [[-4, 4], [-1, 4], [-16, 9]], 0.5, [("wt", b) for b in range(4)], ["ee"])
+    comp("G", 0.2, lambda: [g.iota(T.i64[:, :], [[16, 4]], 0, 1)], [], ["i64"])
     fill(T.onef[:, :], 1.0, 256, ["onef"])
     fill(T.zz[:, :], 0.0, 864, ["z0", "z1", "z2"])
     fill(T.tb[:, P:P + 16], 64.0, 64, ["tbz"])
@@ -156,16 +117,13 @@ def build(g, core, T, topo, rank):
     tt(T.zz[:, 1152 + 15:1728:16], T.e2[:, 36:72], T.ee[:, 108:144], ALU.add, 72, ["ee", "e2b"], ["z2"])
     ts(T.jj[:, 0:1], T.i64[:, 0:1], 4, None, ALU.arith_shift_right, None, 64, ["i64"], ["jj"])
     ts(T.kc[:, 0:1], T.jj[:, 0:1], -1024.0, 8192.0, ALU.mult, ALU.add, 64, ["jj"], ["kc"])
-    ts(T.jc[:, 0:1], T.jj[:, 0:1], 1008.0, None, ALU.mult, None, 64, ["jj"], ["jc"])
-    ts(T.l0[:, :], T.i64[:, :], T.jc[:, 0:1], None, ALU.add, None, 64, ["i64", "jc"], ["l0"])
 
     for s, h in enumerate((1 - mine, mine)):
         peers = [r for r in range(4 * h, 4 * h + 4) if r != rank]
         got = remote([(T.dsrc[r], T.wa[:, BLK * rank:BLK * rank + BLK], r) for r in peers], "arr%d" % s, [("dsrc", h)], ("s", s))
-        arrive("arr%d" % s, got, [("s", s)], wtok(0, 0, peers))
+        node("x", {}, 0.0, None, [("s", s)], wtok(0, 0, peers), sem="arr%d" % s, n=got)
     dma("Y", [(T.wa[:, BLK * rank:BLK * rank + BLK], T.dsrc[rank])], "own", [("dsrc", mine)], wtok(0, 0, [rank]), 65536, 128)
-    comp("G", 0.7, lambda: [g.affine_select(T.rot[:, :], T.onef[:, :], [[0, 2], [-1, 128]], ALU.is_equal, 0.0, 0, 1)],
-         ["onef"], ["rot"])
+    pick(T.rot[:, :], T.onef[:, :], [[0, 2], [-1, 128]], 0.7, ["onef"], ["rot"])
 
     SH, AND = ALU.logical_shift_right, ALU.bitwise_and
     for b, (a1, a2, o1, o2) in enumerate(((8, 71, SH, AND), (11, None, SH, None), (1, 127, SH, AND), (1, None, AND, None))):
@@ -186,7 +144,7 @@ def build(g, core, T, topo, rank):
             def mm(jx=jx, qh=qh, k=k):
                 return [g.tensor.matmul(PR[k][:, 128 * a:128 * a + 128], T.sel[:, 128 * (4 * qh + a):128 * (4 * qh + a) + 128],
                                         T.ht[:, 128 * jx:128 * jx + 128], True, True) for a in range(4)]
-            comp("P", 0.3, mm, ["sel"] + [("ht", b) for b in range(4)], [("pr", k)])
+            comp("P", 0.55 * PE, mm, ["sel"] + [("ht", b) for b in range(4)], [("pr", k)])
             c0 = M * jx + 512 * qh
             copy(T.tb[:, c0:c0 + 512], PR[k][:, :], 512, [], [("pr", k), ("tb", jx, qh)])
     tball = [("tb", jx, qh) for jx in range(N) for qh in range(2)] + ["tbz"]
@@ -194,9 +152,10 @@ def build(g, core, T, topo, rank):
     def lookup(out, c0, offs, o0, rd, tok):
         for h in range(2):
             copy(out[:, c0 + 512 * h:c0 + 512 * h + 512], T.tb[:, 0:P + 16].indirect(offs[:, o0 + 32 * h:o0 + 32 * h + 32]),
-                 512, tball + rd, [(tok, h)], per=1.6)
+                 512, tball + rd, [(tok, h)], per=GAT)
 
-    lookup(T.r0, 0, T.l0, 0, ["l0"], "r0")
+    dma("Y", [(T.r0[16 * j:16 * j + 16, :], T.ht[:, BLK * j:BLK * j + BLK]) for j in range(N)], "r0",
+        [("ht", b) for b in range(4)], [("r0", 0), ("r0", 1)], 262144, 1024)
     PC = [T.pc0, T.pc1]
 
     def deal(d, col, parts, rd):
@@ -207,8 +166,8 @@ def build(g, core, T, topo, rank):
                 for i in range(16):
                     out.append(g.tensor.matmul(PC[d % 2][:, col:col + 64], T.zz[:, z0 + 15 - i:z0 + 143 - i],
                                                buf[:, c0 + i:c0 + M:16], len(out) == 0, len(out) == last))
-            return out
-        comp("P", 0.55 * len(parts), mm, ["z0", "z1", "z2"] + rd, [("pc", d % 2)])
+            return out[-1:]
+        comp("P", PE * len(parts), mm, ["z0", "z1", "z2"] + rd, [("pc", d % 2)])
 
     def lists(d):
         pc, bk = PC[d % 2], ("pc", d % 2)
@@ -234,36 +193,40 @@ def build(g, core, T, topo, rank):
 
     def spread(d):
         b = d % 2
-        w = W[b]
-        ways = CFG["ways"][d]
+        w, ways = W[b], CFG["ways"][d]
         quarter = (2, 3, 0, 1) if d == 0 and mine == 0 else (0, 1, 2, 3)
+
+        def span(lot, k, how):
+            cs = [quarter[t] for t in lot if ways[t][k - 1] == how]
+            return (256 * cs[0], 256 * cs[-1] + 256, range(2 * cs[0], 2 * cs[-1] + 2)) if cs else (0, 0, ())
         for lot in CFG["lots"]:
             pairs, rd, wr, count = [], [], [], 0
             for k in range(1, N):
-                cs = [quarter[t] for t in lot if ways[t][k - 1] == "D"]
-                if cs:
-                    s, c0, c1 = 16 * k, 256 * cs[0], 256 * cs[-1] + 256
+                c0, c1, blks = span(lot, k, "D")
+                if c1:
+                    s = 16 * k
                     pairs.append((w[0:128 - s, M * k + c0:M * k + c1], w[s:128, c0:c1]))
                     pairs.append((w[128 - s:128, M * k + c0:M * k + c1], w[0:s, c0:c1]))
-                    rd += wtok(b, 0, range(c0 // BLK, c1 // BLK))
-                    wr += wtok(b, k, range(c0 // BLK, c1 // BLK))
-                    count += len(cs)
+                    rd += wtok(b, 0, blks)
+                    wr += wtok(b, k, blks)
+                    count += c1 - c0
             if pairs:
-                dma("Y", pairs, "rep%d" % d, sorted(set(rd)), wr, 131072 * count, 64 * len(pairs))
-        for t in range(4):
-            blks, c0 = (2 * quarter[t], 2 * quarter[t] + 1), 256 * quarter[t]
+                dma("Y", pairs, "rep%d" % d, sorted(set(rd)), wr, 512 * count, 64 * len(pairs))
+        for lot in CFG["plots"]:
             for k in range(1, N):
-                if ways[t][k - 1] == "P":
+                c0, c1, blks = span(lot, k, "P")
+                if c1:
                     p = bank()
-                    comp("P", 0.55, lambda k=k, p=p, c0=c0: [g.tensor.matmul(PR[p][:, 0:256], T.rot[:, 16 * k:16 * k + 128],
-                                                                           w[:, c0:c0 + 256], True, True)],
-                         ["rot"] + wtok(b, 0, blks), [("pr", p)])
-                    copy(w[:, M * k + c0:M * k + c0 + 256], PR[p][:, 0:256], 256, [], [("pr", p)] + wtok(b, k, blks))
-                if ways[t][k - 1] == "H":
+                    comp("P", PE * (c1 - c0) / 256, lambda k=k, p=p, c0=c0, c1=c1: [g.tensor.matmul(
+                        PR[p][:, 0:c1 - c0], T.rot[:, 16 * k:16 * k + 128], w[:, c0:c1], True, True)],
+                        ["rot"] + wtok(b, 0, blks), [("pr", p)])
+                    copy(w[:, M * k + c0:M * k + c1], PR[p][:, 0:c1 - c0], c1 - c0, [], [("pr", p)] + wtok(b, k, blks))
+                c0, c1, blks = span(lot, k, "H")
+                if c1:
                     for h in range(2):
-                        copy(w[64 * h:64 * h + 64, M * k + c0:M * k + c0 + 256],
-                             w[64 - 64 * h:128 - 64 * h, M * (k - 4) + c0:M * (k - 4) + c0 + 256], 256,
-                             wtok(b, k - 4, blks, (1 - h,)), wtok(b, k, blks, (h,)), engs=CFG["heng"] if d else "VS")
+                        copy(w[64 * h:64 * h + 64, M * k + c0:M * k + c1],
+                             w[64 - 64 * h:128 - 64 * h, M * (k - 4) + c0:M * (k - 4) + c1], c1 - c0,
+                             wtok(b, k - 4, blks, (1 - h,)), wtok(b, k, blks, (h,)), engs=CFG["heng"][d])
 
     PW = [T.pw0, T.pw1]
 
@@ -273,8 +236,8 @@ def build(g, core, T, topo, rank):
         win = W[b][:, 0:P + 8]
         o1, o2 = 128 * d + c0 // 16, 128 * d + 64 + c0 // 16
         copy(T.ga[:, c0:c0 + n], win.indirect(T.ls[:, o2:o2 + n // 16]), n, wall(b) + [("ls", d)],
-             [("ga", q) for q in blks], per=1.6, engs="S")
-        tt(T.gs[:, c0:c0 + n], win.indirect(T.ls[:, o1:o1 + n // 16]), T.ga[:, c0:c0 + n], ALU.add, 1.6 * n,
+             [("ga", q) for q in blks], per=GAT, engs="S")
+        tt(T.gs[:, c0:c0 + n], win.indirect(T.ls[:, o1:o1 + n // 16]), T.ga[:, c0:c0 + n], ALU.add, GAT * n,
            wall(b) + [("ls", d)] + [("ga", q) for q in blks], [("gs", q) for q in blks], gat=True)
         out, wr = (W[1 - b], wtok(1 - b, 0, blks)) if d < D - 1 else (T.yo, [("yo", q) for q in blks])
         tt(out[:, c0:c0 + n], T.gs[:, c0:c0 + n], PW[c0 // 512][:, c0 % 512:c0 % 512 + n], ALU.subtract, n,
@@ -300,7 +263,7 @@ def build(g, core, T, topo, rank):
         if t < 4:
             got = remote([(T.yf[:, BLK * q:BLK * q + BLK], T.ddst[rank], q) for q in qs], "fa%d" % t,
                          [("yf", q) for q in qs], ("f", t))
-            arrive("fa%d" % t, got, [("f", t)], [("dd", t)])
+            node("x", {}, 0.0, None, [("f", t)], [("dd", t)], sem="fa%d" % t, n=got)
     for t in (4, 0, 1, 2, 3):
         qs = turns[t]
         a, z = qs[0], qs[-1] + 1
@@ -316,19 +279,16 @@ def build(g, core, T, topo, rank):
 
 def plan(ops):
     n = len(ops)
-    deps = [set() for _ in range(n)]
-    soft = [set() for _ in range(n)]
+    deps, soft = [set() for _ in range(n)], [set() for _ in range(n)]
     writer, readers, group = {}, {}, {}
     for i, o in enumerate(ops):
         if o["kind"] == "d":
             group.setdefault(o["sem"], []).append(i)
     for i, o in enumerate(ops):
-        for t in o["rd"]:
+        for t in o["rd"] + o["wr"]:
             if t in writer:
                 deps[i].add(writer[t])
         for t in o["wr"]:
-            if t in writer:
-                deps[i].add(writer[t])
             deps[i].update(readers.get(t, ()))
         for t in o["rd"]:
             readers.setdefault(t, []).append(i)
@@ -341,7 +301,7 @@ def plan(ops):
         for j in list(deps[i]):
             if ops[j]["kind"] == "d":
                 deps[i].update(group[ops[j]["sem"]])
-    tail = {"c": 0.1, "d": 2.0, "r": 2.5, "x": 0.0}
+    tail = {"c": 0.1, "d": CFG["td"], "r": CFG["tr"], "x": 0.0}
     succ = [[] for _ in range(n)]
     for i in range(n):
         for j in sorted(deps[i] | soft[i]):
@@ -409,29 +369,35 @@ def rank_program(g, core, T, topo):
     order, deps, group, _end = plan(ops)
     total = {s: sum(ops[i]["n"] for i in m) for s, m in group.items()}
     count = {e: 0 for e in "VSPG"}
-    done, seen, sent = {}, {}, 0
+    done, sent, waited = {}, 0, {}
+    seen = {e: {} for e in "VSPGY"}
+    known = {}
     for i, e, _t in order:
         o = ops[i]
         if o["kind"] == "x":
             done[i] = (o["sem"], o["n"])
             total[o["sem"]] = o["n"]
             continue
-        need = {}
+        need = {"cG": count["G"]} if e == "G" and o["kind"] == "c" else {}
         for j in deps[i]:
             s, v = done[j]
-            if s == "cP" and e == "P":
-                continue
-            need[s] = max(need.get(s, 0), v)
-        for s in sorted(need):
-            if need[s] > seen.get((e, s), 0):
+            if not (s == "cP" and e == "P"):
+                need[s] = max(need.get(s, 0), v)
+        for s in sorted(need, key=lambda s: (-len(known.get((s, need[s]), ())), s)):
+            if need[s] > seen[e].get(s, 0):
                 Q[e].wait_ge(T.sem[s], need[s])
-                seen[(e, s)] = need[s]
+                seen[e][s] = need[s]
+                waited[s] = max(waited.get(s, 0), need[s])
+                if CFG["trans"]:
+                    for s2, v2 in known.get((s, need[s]), {}).items():
+                        seen[e][s2] = max(seen[e].get(s2, 0), v2)
         ins = o["emit"](e)
         if o["kind"] == "c":
             for x in ins:
                 x.then_inc(T.sem["c" + e], 1)
             count[e] += len(ins)
             done[i] = ("c" + e, count[e])
+            known[done[i]] = dict(seen[e])
         elif o["kind"] == "d":
             for x in ins:
                 x.then_inc(T.sem[o["sem"]], 16)
@@ -442,7 +408,7 @@ def rank_program(g, core, T, topo):
         total["c" + e] = count[e]
     total["sent"] = sent
     for s in sorted(total):
-        if s[:2] != "st" and total[s] > max([v for (_q, x), v in seen.items() if x == s] + [0]):
+        if s[:2] != "st" and total[s] > waited.get(s, 0):
             g.wait_ge(T.sem[s], total[s])
     g.sync.wait_ge(T.sem.st0, total["st0"])
     g.scalar.wait_ge(T.sem.st1, total["st1"])

@@ -1,42 +1,65 @@
+import math
 from concourse.bass import DstId, RemoteDMATransfer
 from concourse.mybir import AluOpType as ALU, ActivationFunctionType as ACT
 
 N, M, D = 8, 1024, 4
-P, BLK = N * M, M // N
-BIG, CC, CLAMP, KEEP = 262144.0, 16384.0, 98304.0, 65536 + 8191
-CFG = {"ways": [["DDDHDDD"] * 4, ["PDDHDDD"] * 4, ["PPDHDDD", "PPDHDDD", "PPDHHDD", "PPDHHDD"], ["PPDHDDD"] * 4],
-       "lots": [[0, 1], [2, 3]], "plots": [[0], [1], [2], [3]], "slope": 20.0, "seed": 0,
-       "noise": 0.0, "heng": ["VSG", "G", "VSG", "VSG"], "trans": False, "rate": 600e3, "row": 0.01, "td": 1.6,
-       "tr": 2.2, "gat": 1.6, "pe": 0.55}
+P = N * M
+UP = 1 << 15
+KEEP = UP * 2 * P + UP + 2 * P - 2
+CFG = {"blocks": [[256, 256, 256, 256]] * 4,
+       "ways": [["DDDDDDD"] * 4, ["DDDHDDD", "DDDHDDD", "PPPHHDD", "PPPHHDD"], ["DDDHDDD", "DDDHDDD", "PPPHHHD", "PPPHHHD"],
+                ["PDDHDDD", "PDDHDDD", "PPPHHHD", "PPPHHHD"]],
+       "lots": [[]] + [[[0, 1], [2, 3]]] * 3, "heng": ["G", "VSG", "VSG", "VSG"], "twice": ["P"] * 3,
+       "turns": [[4, 5], [6, 7], [2, 3], [1]], "stores": [[0, 1], [2], [3]], "frow": 0.038, "look": [256, 512, 512, 512], "hold": True,
+       "lead": [[("S", 0, 128), ("V", 128, 256)], [("S", 0, 256)], [("S", 0, 512)], []],
+       "fill": [[("G", 1024), ("S", 512), ("S", 512), ("V", 2048)], [("S", 512), ("S", 512), ("S", 512), ("V", P)]],
+       "pairs": [[0], [1], [2, 3]], "small": "VS", "heads": [[], [1]], "aff": "VS",
+       "order": ["ld", "seed", "tr", "xr", "own", "tf0", "on", "tb0", "tb1", "remote", "o1", "ab", "ae", "p1", "head00", "head10",
+                 "head11", "a0", "l0", "r0", "a1", "a2", "s0", "l1", "r1", "s1", "l2", "r2", "s2", "s3"], "lag": 0.5,
+       "early": {"su": 8.0}, "rounds": 30000, "heat": 0.006, "seed": 2,
+       "paces": [(1.0, 1.0, 1.0, 1.0, 0.7, 1.6, 53.0), (1.0, 1.0, 1.0, 0.9, 1.6, 2.0, 53.0), (1.38, 1.12, 1.1, 1.1, 1.0, 1.8, 64.0),
+                 (0.75, 0.88, 0.9, 1.1, 1.0, 1.7, 49.0)], "both": ["xr", "tb", "ow", "tr", "st"],
+       "rate": 920e3, "row": 0.023, "td": 1.7, "tr": 1.6, "far": 20e3, "gat": 1.6, "pe": 0.48, "iss": 0.08}
 
-SCRATCH = {"dsrc": ("dram", [N, 128, BLK], "float32"), "ddst": ("dram", [N, 128, BLK], "float32")}
-for _t, _l in (("int32", (("xt", 256), ("xf", M), ("i64", 4), ("jj", 4), ("yi", D * 128))),
-               ("bfloat16", (("hf", M), ("ht", M), ("tb", P + 16), ("r0", M), ("rr", 2 * D * M), ("ones", M), ("sel", M),
-                             ("zz", 12 * 144))),
-               ("uint16", (("off", D * 128), ("ls", D * 128))),
-               ("float32", (("wt", 144), ("ee", 144), ("e2", 72), ("onef", 256), ("rot", 256), ("kc", 4),
-                            ("xa", 3 * D * 64), ("wa", P + 8), ("wb", P + 8), ("ga", M), ("gs", M), ("yo", M), ("yf", M)))):
+SCRATCH = {"tr": ("dram", [D, P], "int32"), "dsrc": ("dram", [N, 128, 128], "float32"), "xin": ("dram", [N, 128, 128], "float32"),
+           "xr": ("sbuf", [128, N, 128], "int32"), "xf": ("sbuf", [128, N, 128], "float32"),
+           "xg": ("sbuf", [128, N, 128], "float32"), "ddst": ("dram", [N, 128, 128], "float32"),
+           "wa": ("sbuf", [128, P + 8], "float32"), "wb": ("sbuf", [128, P + 8], "float32")}
+for _t, _l in (("int32", (("tb", P + 8), ("il", 192), ("i64", 4), ("jj", 4), ("pi", 256), ("y1", 256), ("q1", 256), ("n1", 256),
+                          ("ia", D * 64), ("ib", D * 64), ("ic", D * 64), ("ci", D * 128))),
+               ("uint16", (("off", D * 128), ("ls", D * 128), ("lo", 64))),
+               ("float32", (("ones", 256), ("rot", 256), ("two", 256), ("kc", 4), ("ab", 512), ("ae", 512), ("tz", D * 64),
+                            ("half", 128), ("sel", 128), ("rr", 2 * D * M), ("ga", M), ("gs", M), ("yo", M), ("yf", M)))):
     for _n, _c in _l:
         SCRATCH[_n] = ("sbuf", [128, _c], _t)
-for _n in ("pw0", "pw1", "pr0", "pr1", "pr2", "pr3", "pc0", "pc1"):
+for _n in ("pw0", "pw1", "pr0", "pr1", "pc0", "pc1", "pc2", "pc3"):
     SCRATCH[_n] = ("psum", [128, 512], "float32")
-SEMAPHORES = ["cV", "cS", "cP", "cG", "tree0", "lay", "r0", "ld0", "ld1", "own", "sent", "arr0", "arr1",
-              "rep0", "rep1", "rep2", "rep3", "fa0", "fa1", "fa2", "fa3", "st0", "st1"]
+SEMAPHORES = ["cV", "cS", "cP", "cG", "sent", "arr0", "arr1", "fa0", "fa1", "fa2", "fa3", "fa4", "fa5", "fa6"] + ["d%d" % _i for _i in range(48)]
+KEPT = {}
+
+
+def runs(first, count):
+    first %= N
+    head = min(count, N - first)
+    return [(0, first, head)] + ([(head, 0, count - head)] if count > head else [])
 
 
 def build(g, core, T, topo, rank):
     ops = []
-    Q = {"V": g.vector, "S": g.scalar, "P": g.tensor, "G": g, "Y": g.sync, "A": g.scalar}
-    GAT, PE = CFG["gat"], CFG["pe"]
+    Q = {"V": g.vector, "S": g.scalar, "P": g.tensor, "G": g, "Y": g.sync}
+    GAT, PE = CFG["gat"], CFG["pe"] * 1e-3
+    nsem, stage = [0], ["head"]
 
-    def node(kind, engs, cost, emit, rd, wr, sem=None, n=0, xfer=0.0, gat=False, by=0, rows=0):
-        ops.append({"kind": kind, "engs": engs, "cost": cost, "emit": emit, "rd": list(rd), "wr": list(wr),
-                    "sem": sem, "n": n, "xfer": xfer, "gat": gat, "by": by, "rows": rows})
+    def node(tag, kind, engs, emit, rd, wr, sem=None, n=0, xfer=0.0, par=(), last=False):
+        ops.append({"tag": tag, "kind": kind, "engs": engs, "cost": min(engs.values()) if engs else 0.0, "emit": emit,
+                    "rd": list(rd), "wr": list(wr), "par": list(par), "sem": sem, "n": n, "xfer": xfer, "last": last,
+                    "gat": tag[:2] in ("lk", "ga", "gs", "zo"),
+                    "stage": (CFG["order"] + stage).index(tag if tag in CFG["order"] and stage[0] == "head" else stage[0])})
 
-    def comp(eng, cost, emit, rd, wr, gat=False):
-        node("c", {eng: cost}, cost, lambda e: emit(), rd, wr, gat=gat)
+    def comp(tag, eng, cost, emit, rd, wr):
+        node(tag, "c", {eng: cost}, lambda e: emit(), rd, wr)
 
-    def copy(out, in_, n, rd, wr, per=1.0, scale=None, engs="VS"):
+    def copy(tag, out, in_, n, rd, wr, per=1.0, scale=None, engs="VS"):
         def emit(e):
             if e == "G":
                 return [g.affine_select(out, in_, [[0, n]], ALU.is_ge, 0.0, 0, 0)]
@@ -47,30 +70,45 @@ def build(g, core, T, topo, rank):
             if scale is None:
                 return [g.scalar.activation(out, in_, ACT.Copy)]
             return [g.scalar.activation(out, in_, ACT.Copy, scale=scale)]
-        c = {"V": 0.06 + n * per * 1e-3, "S": 0.075 + n * per * 1e-3, "G": 0.2 + n * 2e-3}
-        node("c", {e: c[e] for e in engs}, c[engs[0]], emit, rd, wr, gat=per > 1)
+        c = {"V": 0.06 + n * per * 1e-3, "S": 0.075 + n * per * 1e-3, "G": 0.32 + n * 2.08e-3}
+        node(tag, "c", {e: c[e] for e in engs}, emit, rd, wr)
 
-    def ts(out, in0, s1, s2, op0, op1, n, rd, wr):
+    def aff(tag, out, in_, scale, bias, n, rd, wr, floor=False):
+        def emit(e):
+            if e == "S":
+                return [g.scalar.activation(out, in_, ACT.Relu if floor else ACT.Identity, bias=bias, scale=scale)]
+            if floor:
+                return [g.vector.tensor_scalar(out, in_, -bias / scale, scale, ALU.is_gt, ALU.mult)]
+            return [g.vector.tensor_scalar(out, in_, scale, bias, ALU.mult, ALU.add)]
+        node(tag, "c", {e: {"V": 0.06, "S": 0.075}[e] + n * 1e-3 for e in CFG["aff"]}, emit, rd, wr)
+
+    def ts(tag, out, in0, s1, s2, op0, op1, n, rd, wr):
         more = [] if op1 is None else [op1]
-        comp("V", 0.06 + n * 1e-3, lambda: [g.vector.tensor_scalar(out, in0, s1, s2, op0, *more)], rd, wr)
+        comp(tag, "V", 0.06 + n * 1e-3, lambda: [g.vector.tensor_scalar(out, in0, s1, s2, op0, *more)], rd, wr)
 
-    def tt(out, a, b, op, cyc, rd, wr, gat=False):
-        comp("V", 0.06 + cyc * 1e-3, lambda: [g.vector.tensor_tensor(out, a, b, op)], rd, wr, gat=gat)
+    def tt(tag, out, a, b, op, cyc, rd, wr):
+        comp(tag, "V", 0.06 + cyc * 1e-3, lambda: [g.vector.tensor_tensor(out, a, b, op)], rd, wr)
 
-    def fill(ap, val, cyc, wr):
-        comp("V", 0.06 + cyc * 1e-3, lambda: [g.vector.memset(ap, val)], [], wr)
+    def fill(ap, val, cyc, wr, tag="fill"):
+        comp(tag, "V", 0.06 + cyc * 1e-3, lambda: [g.vector.memset(ap, val)], [], wr)
 
-    def pick(out, in_, pat, cost, rd, wr):
-        comp("G", cost, lambda: [g.affine_select(out, in_, pat, ALU.is_equal, 0.0, 0, 1)], rd, wr)
+    def pick(out, in_, pat, n, rd, wr):
+        comp("pick", "G", 0.32 + n * 2.08e-3, lambda: [g.affine_select(out, in_, pat, ALU.is_equal, 0.0, 0, 1)], rd, wr)
 
-    def dma(eng, pairs, sem, rd, wr, nbytes, rows):
-        node("d", {"S" if eng == "A" else eng: 0.06 * len(pairs)}, 0.06 * len(pairs),
-             lambda _e: [Q[eng].dma_start(o, i) for o, i in pairs], rd, list(wr) + [("ring", sem)], sem=sem,
-             n=16 * len(pairs), xfer=nbytes / CFG["rate"] + rows * CFG["row"] / 16, by=nbytes, rows=rows)
+    def mms(tag, items, cyc, rd, wr):
+        comp(tag, "P", cyc * PE, lambda: [g.tensor.matmul(*x) for x in items][-1:], rd, wr)
 
-    def remote(items, sem, rd, tok):
+    def dma(tag, pairs, rd, wr, nbytes, rows, par=(), last=False, eng="Y"):
+        nsem[0] += 1
+        node(tag, "d", {e: CFG["iss"] * len(pairs) for e in (eng if tag[:2] not in CFG["both"] else "YS")}, lambda e: [Q[e].dma_start(o, i) for o, i in pairs], rd, wr,
+             sem="d%d" % (nsem[0] - 1), n=16 * len(pairs), xfer=nbytes / CFG["rate"] + rows * CFG["row"] / 16, par=par,
+             last=last)
+
+    def remote(items, sem, rd, tok, nbytes):
         ne = min(len(topo.engines(core, T.cores[r])) for _s, _d, r in items)
-        w = ne // (1 if len(items) == 1 else 2 if len(items) == 2 else 4)
+        w = 1
+        while 2 * w * len(items) <= ne:
+            w *= 2
 
         def emit(_e):
             trs = []
@@ -81,284 +119,408 @@ def build(g, core, T, topo, rank):
                                              remote_sem=T.sem[sem], src=src, dst=dst))
             g.remote_dma_fused(trs, local_sem=T.sem.sent)
             return []
-        node("r", {"G": 0.4}, 0.4, emit, rd, [tok, ("ring", "sent")], sem="sent", n=w * len(items), xfer=128 / w * 0.04,
-             rows=128 / w)
+        node("remote", "r", {"G": 0.4}, emit, rd, [tok, "ring"], sem="sent", n=w * len(items), xfer=nbytes / w / CFG["far"])
         return w * len(items)
 
     W = [T.wa, T.wb]
+    SH, AND = ALU.logical_shift_right, ALU.bitwise_and
 
-    def wtok(b, k, blks, halves=(0, 1)):
-        return [("w", b, k, q, h) for q in blks for h in halves]
+    def wtok(b, k, c0, c1, halves=(0, 1)):
+        return [("w", b, k, q, h) for q in range(c0 // 128, c1 // 128) for h in halves]
+
+    def part(b, k, c0, c1, p0=0, p1=128):
+        return W[b][p0:p1, M * k + c0:M * k + c1]
 
     def wall(b):
-        return [t for k in range(N) for t in wtok(b, k, range(N))] + [("wz", b)]
+        return [t for k in range(N) for t in wtok(b, k, 0, M)] + [("wz", b)]
 
-    dma("A", [(T.xt[:, :], T.tree[rank:rank + 1, :])], "tree0", [], ["xt"], 131072, 128)
-    mine = rank // 4
-    for s, h in enumerate((1 - mine, mine)):
-        dma("Y", [(T.dsrc[4 * h:4 * h + 4, 16 * j:16 * j + 16, :], T.v[64 * h:64 * h + 64, BLK * j:BLK * j + BLK])
-                  for j in range(N)], "ld%d" % s, [], [("dsrc", h)], 262144, 512)
+    waves = [range(1, 5), range(5, 8)]
+    for s, ts_ in enumerate(waves):
+        dma("ld", [(T.dsrc[ts_[0] + o:ts_[0] + o + n], T.v[16 * r:16 * (r + n), :]) for o, r, n in runs(rank + ts_[0], len(ts_))],
+            [], [("dsrc", s)], 65536 * len(ts_), 16)
+    dma("tr", [(T.tr[:], T.tree[rank:rank + 1, :])], [], ["tr"], 131072, 16)
+    c, seed, tbs = 0, P - 512, []
+    fill(T.tb[:, seed:P], 0, 512, [("tf", seed)], "seed")
+    for h, pieces in enumerate(CFG["fill"]):
+        c0, tag = c, "tf%d" % h
+        for e, n in pieces:
+            n, tok = min(n, seed - c), [("tf", c)]
+            if e == "V":
+                fill(T.tb[:, c:c + n], 0, n, tok, tag)
+            elif e == "S":
+                copy(tag, T.tb[:, c:c + n], T.tb[:, seed:seed + n], n, [("tf", seed)], tok, engs="S")
+            else:
+                comp(tag, "G", 0.15 + n * 2e-3, lambda c=c, n=n: [g.iota(T.tb[:, c:c + n], [[1, n]], 0, 0)], [], tok)
+            c += n
+        more = [("tf", seed)] + [t for x in tbs for t in x[2]] if c == seed else []
+        tbs.append((c0, P if more else c, [o["wr"][0] for o in ops[-len(pieces):]] + more))
+    fill(T.tb[:, P:P + 8], 2 * P, 64, ["tbz"])
+    for h in range(4):
+        dma("xr", [(T.xr[8 * d:8 * d + 8, q, :], T.tree[rank:rank + 1, P * d + M * q:P * d + M * q + M])
+                   for d in range(D - 1) for q in range(2 * h, 2 * h + 2)]
+            + [(T.xr[8 * D - 8:8 * D, :, :], T.tree[rank:rank + 1, P * (D - 1):P * D])][h:], [], [("xr", h)], 32768, 64)
+    xr = [("xr", h) for h in range(4)]
+    for h, (c0, c1, toks) in enumerate(tbs):
+        for u in range(2):
+            dma("tb%d" % h, [(T.tb[16 * s:16 * s + D, c0:c1], T.tr[:, c0:c1]) for s in range(4 * u, 4 * u + 4)], ["tr"] + toks, [],
+                64 * (c1 - c0), 16, par=["tb"])
+    comp("lo", "G", 0.4, lambda: [g.iota(T.il[:, 0:64], [[M, N], [16, N]], P, 1)], tbs[-1][2] if CFG["hold"] else [], ["il0"])
+    for s, ts_ in enumerate(waves):
+        got = remote([(T.dsrc[t], T.xin[N - t], (rank + t) % N) for t in ts_], "arr%d" % s,
+                     [("dsrc", s)] + (["il0"] if s and CFG["hold"] else []), ("s", s), 65536)
+        node("arr", "x", {}, None, [("s", s)], [("xin", s)], sem="arr%d" % s, n=got)
 
-    fill(T.ones[:, :], 1.0, 512, ["ones"])
-    pick(T.sel[:, :], T.ones[:, :], [[-1, 8], [0, 8], [-8, 16]], 2.2, ["ones"], ["sel"])
-    for b, val in enumerate((1024.0, 128.0, 1.0, BIG)):
-        fill(T.wt[:, 36 * b:36 * b + 36], val, 64, [("wt", b)])
-    pick(T.ee[:, :], T.wt[:, :], [[-4, 4], [-1, 4], [-16, 9]], 0.5, [("wt", b) for b in range(4)], ["ee"])
-    comp("G", 0.2, lambda: [g.iota(T.i64[:, :], [[16, 4]], 0, 1)], [], ["i64"])
-    fill(T.onef[:, :], 1.0, 256, ["onef"])
-    fill(T.zz[:, :], 0.0, 864, ["z0", "z1", "z2"])
-    fill(T.tb[:, P:P + 16], 64.0, 64, ["tbz"])
+    def slots(tag, src, rel, count, ks, rd):
+        pairs = [(part(0, k, 0, M, 16 * j, 16 * (j + n)), src(rel + o, n))
+                 for k in ks for o, j, n in runs(rank + rel - k, count)]
+        dma(tag, pairs, rd, [], 65536 * count * len(ks), 16 * count * len(ks), par=[t for k in ks for t in wtok(0, k, 0, M)])
+    byd = [0] + [k for k in range(1, N) if CFG["ways"][0][0][k - 1] == "D"]
+    slots("own", lambda r, n: T.v[16 * rank:16 * rank + 16, :], 0, 1, byd, [])
+    for s, ts_ in enumerate(waves):
+        cut = [0] + CFG["heads"][s] + [N]
+        for i in range(len(cut) - 1):
+            slots("head%d%d" % (s, i), lambda r, n: T.xin[r:r + n], N - ts_[-1], len(ts_), byd[cut[i]:cut[i + 1]], [("xin", s)])
+
+    fill(T.ones[:, :], 1.0, 256, ["ones"], "on")
+    fill(T.half[:, 0:128], 0.5, 128, ["half"])
+    fill(T.half[:, 64:128:2], UP / 2, 64, ["half"])
+    pick(T.rot[:, :], T.ones[:, :], [[0, 2], [-1, 128]], 256, ["ones"], ["rot"])
+    for lv in range(2):
+        pick(T.sel[:, 64 * lv:64 * lv + 64], T.half[:, 64 * lv:64 * lv + 64], [[-1, D], [-16, N], [0, 2]], 64, ["half"], ["sel"])
+    comp("i64", "G", 0.15, lambda: [g.iota(T.i64[:, :], [[16, 4]], 0, 1)], [], ["i64"])
+    ts("jj", T.jj[:, 0:1], T.i64[:, 0:1], 4, None, ALU.arith_shift_right, None, 64, ["i64"], ["jj"])
+    ts("kc", T.kc[:, 0:1], T.jj[:, 0:1], -float(M), float(P), ALU.mult, ALU.add, 64, ["jj"], ["kc"])
+    ts("kc2", T.kc[:, 1:2], T.jj[:, 0:1], -2.0 * M, 2.0 * P, ALU.mult, ALU.add, 64, ["jj"], ["kc2"])
+    aff("ab1", T.ab[:, 1:512:2], T.ones[:, :], 0.0, -0.25, 256, ["ones"], ["ab1"])
+    aff("ae1", T.ae[:, 1:512:2], T.ones[:, :], 0.0, T.kc[:, 0:1], 256, ["ones", "kc"], ["ae1"])
+    copy("two", T.two[:, 0:128], T.rot[:, 0:128], 128, ["rot"], ["two"], scale=2.0)
+    copy("six", T.two[:, 128:256], T.rot[:, 0:128], 128, ["rot"], ["six"], scale=0.5 ** D)
+    ts("kc3", T.kc[:, 2:3], T.jj[:, 0:1], 128.0 - 16.0 - M, None, ALU.mult, None, 64, ["jj"], ["kc3"])
+    ts("lo", T.il[:, 64:128], T.il[:, 0:64], T.kc[:, 2:3], None, ALU.add, None, 64, ["il0", "kc3"], ["il1"])
+    ts("lo", T.il[:, 128:192], T.il[:, 64:128], P - 1, None, AND, None, 64, ["il1"], ["il2"])
+    copy("lo", T.lo[:, :], T.il[:, 128:192], 64, ["il2"], ["lo"], engs="V")
     fill(T.wa[:, P:P + 8], 0.0, 64, [("wz", 0)])
     fill(T.wb[:, P:P + 8], 0.0, 64, [("wz", 1)])
-    tt(T.e2[:, 0:36], T.ee[:, 0:36], T.ee[:, 36:72], ALU.add, 72, ["ee"], ["e2a"])
-    tt(T.e2[:, 36:72], T.e2[:, 0:36], T.ee[:, 72:108], ALU.add, 72, ["ee", "e2a"], ["e2b"])
-    copy(T.zz[:, 15:576:16], T.e2[:, 36:72], 64, ["e2b"], ["z0"], engs="V")
-    copy(T.zz[:, 576 + 15:1152:16], T.ee[:, 108:144], 64, ["ee"], ["z1"], engs="V")
-    tt(T.zz[:, 1152 + 15:1728:16], T.e2[:, 36:72], T.ee[:, 108:144], ALU.add, 72, ["ee", "e2b"], ["z2"])
-    ts(T.jj[:, 0:1], T.i64[:, 0:1], 4, None, ALU.arith_shift_right, None, 64, ["i64"], ["jj"])
-    ts(T.kc[:, 0:1], T.jj[:, 0:1], -1024.0, 8192.0, ALU.mult, ALU.add, 64, ["jj"], ["kc"])
 
-    for s, h in enumerate((1 - mine, mine)):
-        peers = [r for r in range(4 * h, 4 * h + 4) if r != rank]
-        got = remote([(T.dsrc[r], T.wa[:, BLK * rank:BLK * rank + BLK], r) for r in peers], "arr%d" % s, [("dsrc", h)], ("s", s))
-        node("x", {}, 0.0, None, [("s", s)], wtok(0, 0, peers), sem="arr%d" % s, n=got)
-    dma("Y", [(T.wa[:, BLK * rank:BLK * rank + BLK], T.dsrc[rank])], "own", [("dsrc", mine)], wtok(0, 0, [rank]), 65536, 128)
-    pick(T.rot[:, :], T.onef[:, :], [[0, 2], [-1, 128]], 0.7, ["onef"], ["rot"])
+    for h in range(2):
+        copy("xf", T.xf[0:32, 4 * h:4 * h + 4, :], T.xr[0:32, 4 * h:4 * h + 4, :], 512, xr, [("xf", h)])
+    for i in range(N):
+        copy("xg", T.xg[0:32, i, :], T.xr[0:32, :, 16 * i:16 * i + 16], 128, xr, [("xg", i)])
+    cf, cb, eye = T.pw0, T.pw1, T.rot[0:32, 0:32]
+    for h in range(2):
+        mms("cf", [(cf[:, i:256:8], T.xg[0:32, i, :], eye, True, True) for i in range(4 * h, 4 * h + 4)], 1024,
+            [("xg", i) for i in range(4 * h, 4 * h + 4)] + ["rot"], [("pw", 0)])
+    for h in range(2):
+        mms("cb", [(cb[:, q:256:8], T.xf[0:32, q, :], eye, True, True) for q in range(4 * h, 4 * h + 4)], 1024,
+            [("xf", h), "rot"], [("pw", 1)])
+    ts("pi", T.pi[:, :], cf[:, 0:256], 0.5, -0.25, ALU.mult, ALU.add, 256, [], [("pw", 0), "pi"])
+    copy("o1", T.off[:, 0:256], T.pi[:, :], 256, ["pi"], ["o1"], engs="V")
+    copy("ab", T.ab[:, 0:512:2], cb[:, 0:256], 256, [], [("pw", 1), "ab0"], scale=-0.5)
+    aff("y1", T.y1[:, :], cf[:, 0:256], 1.0, T.kc[:, 1:2], 256, ["kc2"], [("pw", 0), "y1"])
+    aff("n1", T.n1[:, :], cf[:, 0:256], float(P), -float(P) * (2 * P - 1), 256, [], [("pw", 0), "n1"], floor=True)
+    ts("sf", T.q1[:, :], T.y1[:, :], 1, None, AND, None, 256, ["y1"], ["q1"])
+    aff("ae", T.ae[:, 0:512:2], T.q1[:, :], UP / 2, -UP / 2, 256, ["q1"], ["ae0"])
+    ts("p1", T.y1[:, :], T.y1[:, :], 1, P - 1, SH, AND, 256, ["q1"], ["y1"])
+    tt("p1", T.pi[:, :], T.y1[:, :], T.n1[:, :], ALU.max, 512, ["y1", "n1"], ["pi"])
+    ts("p1", T.ls[:, 0:256], T.pi[:, :], float(P), None, ALU.min, None, 256, ["pi"], ["l1"])
 
-    SH, AND = ALU.logical_shift_right, ALU.bitwise_and
-    for b, (a1, a2, o1, o2) in enumerate(((8, 71, SH, AND), (11, None, SH, None), (1, 127, SH, AND), (1, None, AND, None))):
-        ts(T.xf[:, 256 * b:256 * b + 256], T.xt[:, :], a1, a2, o1, o2, 256, ["xt"], [("xf", b)])
-        copy(T.hf[:, 256 * b:256 * b + 256], T.xf[:, 256 * b:256 * b + 256], 256, [("xf", b)], [("hf", b)])
-        dma("A", [(T.ht[32 * b:32 * b + 32, :], T.hf[:, 256 * b:256 * b + 256])], "lay", [("hf", b)], [("ht", b)], 65536, 128)
-    PR = [T.pr0, T.pr1, T.pr2, T.pr3]
+    PC = [T.pc0, T.pc1, T.pc2, T.pc3]
+
+    def look(ds, lv, bk, first, rd, rd2):
+        pc, n = PC[bk], 128 * len(ds)
+        mms("dl", [(pc[:, 256 * lv:256 * lv + n], T.rot[:, 0:128], first[:, 128 * ds[0]:128 * ds[0] + n], True, False)], 4 * n,
+            ["rot"] + rd2, [("pc", bk)])
+        for d in ds:
+            c0, o0, col, s0 = M * (2 * d + lv), 256 * lv + 64 * d, 256 * lv + 128 * (d - ds[0]), 64 * lv + 16 * d
+            n = CFG["look"][d]
+            for h in range(M // n):
+                copy("lk%d%d" % (d, lv), T.rr[:, c0 + n * h:c0 + n * h + n],
+                     T.tb[:, 0:P + 8].indirect(T.off[:, o0 + n // 16 * h:o0 + n // 16 * (h + 1)]), n, ["tb", "tbz"] + rd,
+                     [("r", d, lv, h)], per=GAT)
+                mms("dl%d%d" % (d, lv),
+                    [(pc[:, col + 16 * a:col + 16 * a + 16], T.rr[:, c0 + 128 * a:c0 + 128 * a + 128], T.sel[:, s0:s0 + 16],
+                      False, a == N - 1 and d == ds[-1]) for a in range(n // 128 * h, n // 128 * (h + 1))],
+                    2 * n, ["sel", ("r", d, lv, h)], [("pc", bk)])
+
+    def lists(i, ds):
+        d, n = ds[0], 64 * len(ds)
+        x, bk = slice(64 * d, 64 * d + n), ("pc", i)
+        even, odd = PC[i][:, 0:2 * n:2], PC[i][:, 1:2 * n:2]
+        look(ds, 0, i, T.ab, ["o1"], ["ab0", "ab1"])
+        copy("z1", T.ia[:, x], even, n, [], [bk, ("ia", d)], scale=2.0, engs=CFG["small"])
+        ts("z2", T.ib[:, x], T.ia[:, x], 1, None, AND, None, n, [("ia", d)], [("ib", d)])
+        tt("z3", T.tz[:, x], T.ib[:, x], even, ALU.mult, n, [("ib", d)], [bk, ("tz", d)])
+        tt("z4", T.ic[:, x], odd, T.tz[:, x], ALU.subtract, n, [("tz", d)], [bk, ("ic", d)])
+        copy("z5", T.off[:, 256 + 64 * d:256 + 64 * d + n], T.ic[:, x], n, [("ic", d)], [("o2", d)], engs="V")
+        stage[0] = "l%d" % d
+        look(ds, 1, i, T.ae, [("o2", d)], ["ae0", "ae1"])
+        c0, c1 = 128 * d, 128 * d + 2 * n
+        copy("f1", T.ci[:, c0:c1], PC[i][:, 256:256 + 2 * n], 2 * n, [], [bk, ("ci", d)], scale=2.0, engs=CFG["small"])
+        ts("f2", T.ci[:, c0:c1], T.ci[:, c0:c1], KEEP, None, AND, None, 2 * n, [], [("ci", d)])
+        tt("f3", T.ic[:, x], T.ci[:, c0:c1:2], T.ci[:, c0 + 1:c1:2], ALU.max, 2 * n, [("ci", d)], [("ic", d)])
+        ts("ls%d" % d, T.ls[:, 256 + 64 * d:256 + 64 * d + n], T.ic[:, x], 0.5, float(P), ALU.mult, ALU.min, n, [("ic", d)],
+           [("l2", e) for e in ds])
+
     nb = [0]
 
-    def bank():
+    def bank(d):
+        pool = [(T.pr0, ("pr", 0)), (T.pr1, ("pr", 1))] + [(PC[i], ("pc", i)) for i in range(D) if max((CFG["pairs"] + [[-1]] * D)[i]) < d]
         nb[0] += 1
-        return (nb[0] - 1) % 4
+        return pool[nb[0] % len(pool)]
 
-    for jx in range(N):
-        for qh in range(2):
-            k = bank()
-
-            def mm(jx=jx, qh=qh, k=k):
-                return [g.tensor.matmul(PR[k][:, 128 * a:128 * a + 128], T.sel[:, 128 * (4 * qh + a):128 * (4 * qh + a) + 128],
-                                        T.ht[:, 128 * jx:128 * jx + 128], True, True) for a in range(4)]
-            comp("P", 0.55 * PE, mm, ["sel"] + [("ht", b) for b in range(4)], [("pr", k)])
-            c0 = M * jx + 512 * qh
-            copy(T.tb[:, c0:c0 + 512], PR[k][:, :], 512, [], [("pr", k), ("tb", jx, qh)])
-    tball = [("tb", jx, qh) for jx in range(N) for qh in range(2)] + ["tbz"]
-
-    def lookup(out, c0, offs, o0, rd, tok):
-        for h in range(2):
-            copy(out[:, c0 + 512 * h:c0 + 512 * h + 512], T.tb[:, 0:P + 16].indirect(offs[:, o0 + 32 * h:o0 + 32 * h + 32]),
-                 512, tball + rd, [(tok, h)], per=GAT)
-
-    dma("Y", [(T.r0[16 * j:16 * j + 16, :], T.ht[:, BLK * j:BLK * j + BLK]) for j in range(N)], "r0",
-        [("ht", b) for b in range(4)], [("r0", 0), ("r0", 1)], 262144, 1024)
-    PC = [T.pc0, T.pc1]
-
-    def deal(d, col, parts, rd):
-        def mm():
-            out, last = [], 16 * len(parts) - 1
-            for kind, buf, c0 in parts:
-                z0 = 144 * (4 * kind + d)
-                for i in range(16):
-                    out.append(g.tensor.matmul(PC[d % 2][:, col:col + 64], T.zz[:, z0 + 15 - i:z0 + 143 - i],
-                                               buf[:, c0 + i:c0 + M:16], len(out) == 0, len(out) == last))
-            return out[-1:]
-        comp("P", PE * len(parts), mm, ["z0", "z1", "z2"] + rd, [("pc", d % 2)])
-
-    def lists(d):
-        pc, bk = PC[d % 2], ("pc", d % 2)
-        o1, o2, c1, c2 = 128 * d, 128 * d + 64, 2 * M * d, 2 * M * d + M
-        r0, r1, r2 = [("r0", 0), ("r0", 1)], [(("r1", d), 0), (("r1", d), 1)], [(("r2", d), 0), (("r2", d), 1)]
-        deal(d, 0, [(0, T.r0, 0)], r0)
-        ts(T.off[:, o1:o1 + 64], pc[:, 0:64], float(P), None, ALU.min, None, 64, [], [bk, ("o1", d)])
-        ts(T.yi[:, o1:o1 + 64], pc[:, 0:64], T.kc[:, 0:1], None, ALU.add, None, 64, ["kc"], [bk, ("y1", d)])
-        lookup(T.rr, c1, T.off, o1, [("o1", d)], ("r1", d))
-        deal(d, 64, [(0, T.rr, c1)], r1)
-        ts(T.off[:, o2:o2 + 64], pc[:, 64:128], float(P), None, ALU.min, None, 64, [], [bk, ("o2", d)])
-        lookup(T.rr, c2, T.off, o2, [("o2", d)], ("r2", d))
-        x = 192 * d
-        deal(d, 128, [(1, T.r0, 0), (2, T.rr, c1)], r0 + r1)
-        comp("S", 0.14, lambda: [g.scalar.activation(T.xa[:, x:x + 64], pc[:, 128:192], ACT.Abs, bias=-BIG)], [], [bk, ("x1", d)])
-        deal(d, 192, [(1, T.r0, 0), (2, T.rr, c2)], r0 + r2)
-        comp("S", 0.14, lambda: [g.scalar.activation(T.xa[:, x + 64:x + 128], pc[:, 192:256], ACT.Abs, bias=CC - BIG)],
-             [], [bk, ("x2", d)])
-        tt(T.xa[:, x + 128:x + 192], T.xa[:, x:x + 64], T.xa[:, x + 64:x + 128], ALU.min, 128, [("x1", d), ("x2", d)], [("x3", d)])
-        ts(T.yi[:, o2:o2 + 64], T.xa[:, x + 128:x + 192], CLAMP, T.kc[:, 0:1], ALU.min, ALU.add, 64, [("x3", d), "kc"], [("y2", d)])
-        ts(T.yi[:, o1:o1 + 128], T.yi[:, o1:o1 + 128], KEEP, None, AND, None, 128, [], [("y1", d), ("y2", d)])
-        ts(T.ls[:, o1:o1 + 128], T.yi[:, o1:o1 + 128], float(P), None, ALU.min, None, 128, [("y1", d), ("y2", d)], [("ls", d)])
+    def edges(d):
+        out = [0]
+        for n in CFG["blocks"][d]:
+            out.append(out[-1] + n)
+        return out
 
     def spread(d):
-        b = d % 2
-        w, ways = W[b], CFG["ways"][d]
-        quarter = (2, 3, 0, 1) if d == 0 and mine == 0 else (0, 1, 2, 3)
-
-        def span(lot, k, how):
-            cs = [quarter[t] for t in lot if ways[t][k - 1] == how]
-            return (256 * cs[0], 256 * cs[-1] + 256, range(2 * cs[0], 2 * cs[-1] + 2)) if cs else (0, 0, ())
-        for lot in CFG["lots"]:
+        b, e = d % 2, edges(d - 1)
+        ways = CFG["ways"][d]
+        for lot in CFG["lots"][d]:
             pairs, rd, wr, count = [], [], [], 0
             for k in range(1, N):
-                c0, c1, blks = span(lot, k, "D")
-                if c1:
-                    s = 16 * k
-                    pairs.append((w[0:128 - s, M * k + c0:M * k + c1], w[s:128, c0:c1]))
-                    pairs.append((w[128 - s:128, M * k + c0:M * k + c1], w[0:s, c0:c1]))
-                    rd += wtok(b, 0, blks)
-                    wr += wtok(b, k, blks)
+                cs = [t for t in lot if ways[t][k - 1] == "D"]
+                if cs:
+                    c0, c1, s = e[cs[0]], e[cs[-1] + 1], 16 * k
+                    pairs.append((part(b, k, c0, c1, 0, 128 - s), part(b, 0, c0, c1, s, 128)))
+                    pairs.append((part(b, k, c0, c1, 128 - s, 128), part(b, 0, c0, c1, 0, s)))
+                    rd += wtok(b, 0, c0, c1)
+                    wr += wtok(b, k, c0, c1)
                     count += c1 - c0
             if pairs:
-                dma("Y", pairs, "rep%d" % d, sorted(set(rd)), wr, 512 * count, 64 * len(pairs))
-        for lot in CFG["plots"]:
+                dma("rep%d" % d, pairs, sorted(set(rd)), wr, 512 * count, 64 * len(pairs))
+        for t in range(len(ways)):
+            c0, c1 = e[t], e[t + 1]
+            n = c1 - c0
             for k in range(1, N):
-                c0, c1, blks = span(lot, k, "P")
-                if c1:
-                    p = bank()
-                    comp("P", PE * (c1 - c0) / 256, lambda k=k, p=p, c0=c0, c1=c1: [g.tensor.matmul(
-                        PR[p][:, 0:c1 - c0], T.rot[:, 16 * k:16 * k + 128], w[:, c0:c1], True, True)],
-                        ["rot"] + wtok(b, 0, blks), [("pr", p)])
-                    copy(w[:, M * k + c0:M * k + c1], PR[p][:, 0:c1 - c0], c1 - c0, [], [("pr", p)] + wtok(b, k, blks))
-                c0, c1, blks = span(lot, k, "H")
-                if c1:
+                if ways[t][k - 1] == "P":
+                    pr, bk = bank(d)
+                    mms("rot", [(pr[:, 0:n], T.rot[:, 16 * k:16 * k + 128], part(b, 0, c0, c1), True, True)], 4 * n,
+                        ["rot"] + wtok(b, 0, c0, c1), [bk])
+                    copy("pc", part(b, k, c0, c1), pr[:, 0:n], n, [], [bk] + wtok(b, k, c0, c1))
+                if ways[t][k - 1] == "H":
                     for h in range(2):
-                        copy(w[64 * h:64 * h + 64, M * k + c0:M * k + c1],
-                             w[64 - 64 * h:128 - 64 * h, M * (k - 4) + c0:M * (k - 4) + c1], c1 - c0,
-                             wtok(b, k - 4, blks, (1 - h,)), wtok(b, k, blks, (h,)), engs=CFG["heng"][d])
+                        copy("hc", part(b, k, c0, c1, 64 * h, 64 * h + 64), part(b, k - 4, c0, c1, 64 - 64 * h, 128 - 64 * h), n,
+                             wtok(b, k - 4, c0, c1, (1 - h,)), wtok(b, k, c0, c1, (h,)), engs=CFG["heng"][d])
 
     PW = [T.pw0, T.pw1]
 
-    def step(d, c0, n):
-        b = d % 2
-        blks = range(c0 // BLK, (c0 + n) // BLK)
+    def step(d, c0, c1, lead):
+        b, n = d % 2, c1 - c0
+        blks = range(c0 // 128, c1 // 128)
         win = W[b][:, 0:P + 8]
-        o1, o2 = 128 * d + c0 // 16, 128 * d + 64 + c0 // 16
-        copy(T.ga[:, c0:c0 + n], win.indirect(T.ls[:, o2:o2 + n // 16]), n, wall(b) + [("ls", d)],
-             [("ga", q) for q in blks], per=GAT, engs="S")
-        tt(T.gs[:, c0:c0 + n], win.indirect(T.ls[:, o1:o1 + n // 16]), T.ga[:, c0:c0 + n], ALU.add, GAT * n,
-           wall(b) + [("ls", d)] + [("ga", q) for q in blks], [("gs", q) for q in blks], gat=True)
-        out, wr = (W[1 - b], wtok(1 - b, 0, blks)) if d < D - 1 else (T.yo, [("yo", q) for q in blks])
-        tt(out[:, c0:c0 + n], T.gs[:, c0:c0 + n], PW[c0 // 512][:, c0 % 512:c0 % 512 + n], ALU.subtract, n,
-           [("gs", q) for q in blks], wr + [("pw", c0 // 512)])
-
-    for d in range(D):
-        lists(d)
-    for d in range(D):
-        spread(d)
-        for h in range(2):
-            copy(PW[h][:, :], W[d % 2][:, 512 * h:512 * h + 512], 512, wtok(d % 2, 0, range(4 * h, 4 * h + 4)), [("pw", h)],
-                 scale=2.0)
+        o1, o2 = 64 * d + c0 // 16, 256 + 64 * d + c0 // 16
+        for e, x0, x1 in lead:
+            copy("ga%d" % d, T.ga[:, c0 + x0:c0 + x1], win.indirect(T.ls[:, o2 + x0 // 16:o2 + x1 // 16]), x1 - x0,
+                 wall(b) + [("l2", d)], [("ga", q) for q in range((c0 + x0) // 128, (c0 + x1) // 128)], per=GAT, engs=e)
+        tt("gs", T.gs[:, c0:c1], win.indirect(T.ls[:, o1:o1 + n // 16]), T.ga[:, c0:c1], ALU.add, GAT * n,
+           wall(b) + ["l1"] + [("ga", q) for q in blks], [("gs", q) for q in blks])
         if d < D - 1:
-            for c in range(4):
-                step(d, 256 * c, 256)
+            tt("su%d" % d, part(1 - b, 0, c0, c1), PW[c0 // 512][:, c0 % 512:c0 % 512 + n], T.gs[:, c0:c1], ALU.subtract, n,
+               [("gs", q) for q in blks], wtok(1 - b, 0, c0, c1) + [("pw", c0 // 512)])
+            return
+        pr, bk = bank(d)
+        copy("zo", T.yo[:, c0:c1], win.indirect(T.lo[:, c0 // 16:c1 // 16]), n, wall(b) + ["lo"], [("yo", q) for q in blks],
+             per=GAT, scale=0.5 ** d)
+        mms("hv", [(pr[:, 0:n], T.two[:, 128:256], T.gs[:, c0:c1], True, True)], 4 * n, ["six"] + [("gs", q) for q in blks], [bk])
+        tt("su%d" % d, T.yf[:, c0:c1], T.yo[:, c0:c1], pr[:, 0:n], ALU.subtract, n, [("yo", q) for q in blks],
+           [bk] + [("yf", q) for q in blks])
 
-    pair = rank // 2
-    turns = [[2 * (pair ^ t), 2 * (pair ^ t) + 1] for t in (1, 2, 3)] + [[rank ^ 1], [rank]]
-    for t, qs in enumerate(turns):
-        c0, n = BLK * qs[0], BLK * len(qs)
-        step(D - 1, c0, n)
-        copy(T.yf[:, c0:c0 + n], T.yo[:, c0:c0 + n], n, [("yo", q) for q in qs], [("yf", q) for q in qs], scale=0.0625, engs="S")
-        if t < 4:
-            got = remote([(T.yf[:, BLK * q:BLK * q + BLK], T.ddst[rank], q) for q in qs], "fa%d" % t,
-                         [("yf", q) for q in qs], ("f", t))
-            node("x", {}, 0.0, None, [("f", t)], [("dd", t)], sem="fa%d" % t, n=got)
-    for t in (4, 0, 1, 2, 3):
-        qs = turns[t]
-        a, z = qs[0], qs[-1] + 1
-        for e, js in (("Y", range(0, 4)), ("A", range(4, 8))):
-            if t < 4:
-                src, rd = [T.ddst[a:z, 16 * j:16 * j + 16, :] for j in js], [("dd", t)]
+    for i, ds in enumerate(CFG["pairs"]):
+        stage[0] = "a%d" % ds[0]
+        lists(i, ds)
+    for d in range(D - 1):
+        stage[0] = "r%d" % d
+        spread(d)
+        stage[0] = "s%d" % d
+        for h in range(2):
+            src, rd = part(d % 2, 0, 512 * h, 512 * h + 512), wtok(d % 2, 0, 512 * h, 512 * h + 512)
+            if CFG["twice"][d] == "P":
+                mms("tw", [(PW[h][:, :], T.two[:, 0:128], src, True, True)], 2048, rd + ["two"], [("pw", h)])
             else:
-                src, rd = [T.yf[16 * j:16 * j + 16, BLK * a:BLK * z] for j in js], [("yf", a)]
-            dma(e, [(T.y[16 * a:16 * z, BLK * j:BLK * j + BLK], s) for j, s in zip(js, src)], "st0" if e == "Y" else "st1",
-                rd, [], 32768 * len(qs), 64 * len(qs))
+                copy("tw", PW[h][:, :], src, 512, rd, [("pw", h)], scale=2.0)
+        e = edges(d)
+        for t in range(len(e) - 1):
+            step(d, e[t], e[t + 1], CFG["lead"][t])
+
+    stage[0] = "r%d" % (D - 1)
+    spread(D - 1)
+    stage[0] = "s%d" % (D - 1)
+    turns = [sorted(rank ^ x for x in xs) for xs in CFG["turns"]] + [[rank]]
+    nt = len(turns) - 1
+    for t, qs in enumerate(turns):
+        step(D - 1, 128 * qs[0], 128 * qs[-1] + 128, [("S", 0, 128 * len(qs))])
+        if t < nt:
+            got = remote([(T.yf[:, 128 * q:128 * q + 128], T.ddst[rank], q) for q in qs], "fa%d" % t,
+                         [("yf", q) for q in qs], ("f", t), 128 * CFG["frow"] * CFG["far"])
+            node("arr", "x", {}, None, [("f", t)], [("dd", t)], sem="fa%d" % t, n=got)
+    for lot in [[nt]] + CFG["stores"]:
+        a, z = min(turns[t][0] for t in lot), max(turns[t][-1] for t in lot) + 1
+        for e, js in (("Y", range(0, 4)), ("S", range(4, 8))):
+            if lot[0] < nt:
+                src, rd = [T.ddst[a:z, 16 * j:16 * j + 16, :] for j in js], [("dd", t) for t in lot]
+            else:
+                src, rd = [T.yf[16 * j:16 * j + 16, 128 * a:128 * z] for j in js], [("yf", a)]
+            dma("st", [(T.y[16 * a:16 * z, 128 * j:128 * j + 128], s) for j, s in zip(js, src)], rd, [], 32768 * (z - a),
+                64 * (z - a), last=True, eng=e)
     return ops, Q
 
 
 def plan(ops):
     n = len(ops)
     deps, soft = [set() for _ in range(n)], [set() for _ in range(n)]
-    writer, readers, group = {}, {}, {}
-    for i, o in enumerate(ops):
-        if o["kind"] == "d":
-            group.setdefault(o["sem"], []).append(i)
+    writer, readers = {}, {}
     for i, o in enumerate(ops):
         for t in o["rd"] + o["wr"]:
-            if t in writer:
-                deps[i].add(writer[t])
-        for t in o["wr"]:
+            deps[i].update(writer.get(t, ()))
+        for t in o["wr"] + o["par"]:
             deps[i].update(readers.get(t, ()))
         for t in o["rd"]:
             readers.setdefault(t, []).append(i)
         for t in o["wr"]:
-            writer[t] = i
+            writer[t] = [i]
             readers[t] = []
+        for t in o["par"]:
+            writer.setdefault(t, []).append(i)
         deps[i].discard(i)
-        soft[i] = {j for j in deps[i] if o["kind"] in "dr" and ops[j]["kind"] == o["kind"] and ops[j]["sem"] == o["sem"]}
+        soft[i] = {j for j in deps[i] if o["kind"] == "r" and ops[j]["kind"] == "r"}
         deps[i] -= soft[i]
-        for j in list(deps[i]):
-            if ops[j]["kind"] == "d":
-                deps[i].update(group[ops[j]["sem"]])
     tail = {"c": 0.1, "d": CFG["td"], "r": CFG["tr"], "x": 0.0}
     succ = [[] for _ in range(n)]
     for i in range(n):
         for j in sorted(deps[i] | soft[i]):
             succ[j].append(i)
     prio = [0.0] * n
-    todo = [len(s) for s in succ]
-    stack = [i for i in range(n) if todo[i] == 0]
-    while stack:
-        i = stack.pop()
+    for i in range(n - 1, -1, -1):
         prio[i] = ops[i]["cost"] + ops[i]["xfer"] + max(
             [prio[k] + (0.0 if i in soft[k] else tail[ops[i]["kind"]]) for k in succ[i]] + [tail[ops[i]["kind"]]])
-        for j in deps[i] | soft[i]:
-            todo[j] -= 1
-            if todo[j] == 0:
-                stack.append(j)
-    x = CFG["seed"]
-    for i in range(n):
-        x = (x * 1103515245 + 12345) % 2147483648
-        prio[i] += CFG["noise"] * (x / 2147483648.0)
-    prio[0] += 100.0
-    left = [len(deps[i] | soft[i]) for i in range(n)]
-    ready = [i for i in range(n) if left[i] == 0]
-    free = {e: 0.0 for e in "VSPGY"}
-    rings = [0.0, 0.0]
-    end, order = [0.0] * n, []
-    while ready:
-        cand = []
-        for i in ready:
-            t0 = max([end[j] for j in deps[i]] + [0.0])
-            if ops[i]["kind"] == "x":
-                cand = [(t0, i, None)]
+    stage = [o["stage"] for o in ops]
+    for i in range(n - 1, -1, -1):
+        stage[i] = min([stage[i]] + [stage[k] for k in succ[i]])
+        prio[i] += CFG["early"].get(ops[i]["tag"][:2], 0.0)
+        prio[i] = max([prio[i]] + [prio[k] + 1e-6 for k in succ[i] if stage[k] == stage[i]])
+
+    def gap(busy, t, c):
+        for a, z in busy:
+            if a - t >= c - 1e-9:
                 break
-            e = min(ops[i]["engs"], key=lambda x: (max(t0, free[x]) + ops[i]["engs"][x], x))
-            cand.append((max(t0, free[e]), i, e))
-        first = min(c[0] for c in cand)
-        t0, i, e = max(cand, key=lambda c: (prio[c[1]] - CFG["slope"] * max(c[0] - first - 0.1, 0.0), -c[1]))
-        o = ops[i]
-        if e is None:
-            end[i] = t0
+            t = max(t, z)
+        return t
+
+    busy = {e: [] for e in "VSPGYdr"}
+    end, qend, start, eng = [0.0] * n, [0.0] * n, [0.0] * n, [None] * n
+    for i in sorted(range(n), key=lambda i: (stage[i], -prio[i], i)):
+        o, k = ops[i], ops[i]["kind"]
+        t0 = max([end[j] for j in deps[i]] + [qend[j] for j in soft[i]] + [0.0])
+        if k == "x":
+            start[i] = end[i] = t0
+            continue
+        while True:
+            t, e = min((gap(busy[x], t0, c) + c, x) for x, c in o["engs"].items())
+            t1 = t - o["engs"][e] + CFG["iss"]
+            if k != "d" or gap(busy[k], t1, o["xfer"]) <= t1 + CFG["lag"] + 1e-6:
+                break
+            t0 = gap(busy[k], t1, o["xfer"]) - CFG["iss"] - CFG["lag"]
+        start[i], qend[i], eng[i] = t - o["engs"][e], t, e
+        busy[e] = sorted(busy[e] + [(start[i], t)])
+        if k != "c":
+            t1 = gap(busy["d"], start[i] + CFG["iss"] if k == "d" else t, o["xfer"])
+            busy["d"] = sorted(busy["d"] + [(t1, t1 + o["xfer"])])
+            t = max(t, t1 + o["xfer"])
+        end[i] = t + tail[k]
+    before = [deps[i] | soft[i] for i in range(n)]
+    if "order" not in KEPT:
+        KEPT["order"], KEPT["eng"] = polish(ops, sorted(range(n), key=lambda i: (start[i], i)), eng, deps, before)
+    todo, order, placed = list(KEPT["order"]), [], set()
+    while todo:
+        i = next(x for x in todo if before[x] <= placed)
+        todo.remove(i)
+        placed.add(i)
+        order.append((i, KEPT["eng"][i], start[i]))
+    return order, deps, end
+
+
+def polish(ops, order, eng, deps, before):
+    n = len(ops)
+    kind, pe = [o["kind"] for o in ops], ["P" in o["engs"] for o in ops]
+    paces = []
+    for gat, vec, ten, ring, iss, td, unit in CFG["paces"]:
+        f = [iss if o["kind"] == "d" else 1.0 if o["kind"] != "c" else ten if "P" in o["engs"] else gat if o["gat"] else vec
+             for o in ops]
+        paces.append(([{e: c * f[i] for e, c in o["engs"].items()} for i, o in enumerate(ops)], [o["xfer"] * ring for o in ops],
+                      {"c": 0.1, "d": td, "r": CFG["tr"], "i": iss * CFG["iss"]}, unit))
+
+    def run(order, eng, pace):
+        cost, xfer, tail, unit = pace
+        free, last = dict.fromkeys("VSPGYdr", 0.0), {}
+        end, by = [0.0] * n, [(-1, False)] * n
+        for i in order:
+            e, k, t, b = eng[i], kind[i], 0.0, (-1, False)
+            for j in deps[i]:
+                x = end[j] - 0.1 if pe[i] and pe[j] else end[j]
+                if x > t:
+                    t, b = x, (j, False)
+            if e is not None:
+                if free[e] > t:
+                    t, b = free[e], (last[e], True)
+                t0, t = t, t + cost[i][e]
+                free[e], last[e] = t, i
+                if k != "c":
+                    t0 = t0 + tail["i"] if k == "d" else t
+                    if free["d"] > t0:
+                        t0, b = free["d"], (last["d"], True)
+                    free["d"], last["d"] = t0 + xfer[i], i
+                    t = max(t, free["d"])
+                t += tail[k]
+            end[i], by[i] = t, b
+        i, chain = end.index(max(end)), []
+        while i >= 0:
+            chain.append((i,) + by[i])
+            i = by[i][0]
+        return (max(end) / unit) ** 4, chain
+
+    seed = [CFG["seed"]]
+
+    def rnd():
+        seed[0] = (seed[0] * 1103515245 + 12345) % 2147483648
+        return seed[0] / 2147483648.0
+
+    now = [run(order, eng, p) for p in paces]
+    best = (sum(r[0] for r in now), order, eng)
+    for it in range(CFG["rounds"]):
+        chain = now[int(rnd() * len(now))][1]
+        i, j, queued = chain[int(rnd() * len(chain))]
+        new, e2, r = order, eng, rnd()
+        if r < 0.3:
+            x = i if r < 0.15 or j < 0 else j
+            other = [y for y in ops[x]["engs"] if y != eng[x]]
+            if not other:
+                continue
+            e2 = list(eng)
+            e2[x] = other[int(rnd() * len(other))]
         else:
-            free[e] = t0 + o["engs"][e]
-            if o["kind"] == "c":
-                end[i] = free[e] + tail["c"]
-            elif o["kind"] == "d":
-                rings[0] = max(rings[0], t0 + 0.06) + o["xfer"]
-                end[i] = max(rings[0], free[e]) + tail["d"]
-            else:
-                rings[1] = max(rings[1], free[e]) + o["xfer"]
-                rings[0] = max(rings[0], free[e]) + 0.3 * o["xfer"]
-                end[i] = rings[1] + tail["r"]
-        order.append((i, e, t0))
-        ready.remove(i)
-        for k in succ[i]:
-            left[k] -= 1
-            if left[k] == 0:
-                ready.append(k)
-    return order, deps, group, end
+            if r < 0.4:
+                i = int(rnd() * n)
+                j = next((x for x in reversed(order[:order.index(i)]) if eng[x] == eng[i]), -1)
+                queued = j >= 0 and eng[i] is not None
+            if not queued:
+                continue
+            p, q = order.index(i), order.index(j)
+            span, need = order[q:p + 1], {i}
+            for x in reversed(span):
+                if x in need:
+                    need |= before[x]
+            if j in need:
+                continue
+            new = order[:q] + [x for x in span if x in need] + [x for x in span if x not in need] + order[p + 1:]
+        then = [run(new, e2, p) for p in paces]
+        worse = sum(r[0] for r in then) - sum(r[0] for r in now)
+        if worse <= 0 or rnd() < math.exp(-worse / (CFG["heat"] * (1.001 - it / CFG["rounds"]))):
+            order, eng, now = new, e2, then
+            if sum(r[0] for r in now) < best[0]:
+                best = (sum(r[0] for r in now), order, eng)
+    return best[1], best[2]
 
 
 def rank_program(g, core, T, topo):
@@ -366,12 +528,10 @@ def rank_program(g, core, T, topo):
     if rank is None:
         return
     ops, Q = build(g, core, T, topo, rank)
-    order, deps, group, _end = plan(ops)
-    total = {s: sum(ops[i]["n"] for i in m) for s, m in group.items()}
+    order, deps, _end = plan(ops)
     count = {e: 0 for e in "VSPG"}
-    done, sent, waited = {}, 0, {}
+    done, total, waited, last = {}, {"sent": 0}, {}, []
     seen = {e: {} for e in "VSPGY"}
-    known = {}
     for i, e, _t in order:
         o = ops[i]
         if o["kind"] == "x":
@@ -383,32 +543,31 @@ def rank_program(g, core, T, topo):
             s, v = done[j]
             if not (s == "cP" and e == "P"):
                 need[s] = max(need.get(s, 0), v)
-        for s in sorted(need, key=lambda s: (-len(known.get((s, need[s]), ())), s)):
+        for s in sorted(need):
             if need[s] > seen[e].get(s, 0):
                 Q[e].wait_ge(T.sem[s], need[s])
                 seen[e][s] = need[s]
                 waited[s] = max(waited.get(s, 0), need[s])
-                if CFG["trans"]:
-                    for s2, v2 in known.get((s, need[s]), {}).items():
-                        seen[e][s2] = max(seen[e].get(s2, 0), v2)
         ins = o["emit"](e)
         if o["kind"] == "c":
             for x in ins:
                 x.then_inc(T.sem["c" + e], 1)
             count[e] += len(ins)
             done[i] = ("c" + e, count[e])
-            known[done[i]] = dict(seen[e])
         elif o["kind"] == "d":
             for x in ins:
                 x.then_inc(T.sem[o["sem"]], 16)
-            done[i] = (o["sem"], total[o["sem"]])
+            done[i] = (o["sem"], o["n"])
+            if o["last"]:
+                last.append((e, o["sem"], o["n"]))
+            else:
+                total[o["sem"]] = o["n"]
         else:
-            sent += o["n"]
+            total["sent"] += o["n"]
     for e in "VSPG":
         total["c" + e] = count[e]
-    total["sent"] = sent
     for s in sorted(total):
-        if s[:2] != "st" and total[s] > waited.get(s, 0):
+        if total[s] > waited.get(s, 0):
             g.wait_ge(T.sem[s], total[s])
-    g.sync.wait_ge(T.sem.st0, total["st0"])
-    g.scalar.wait_ge(T.sem.st1, total["st1"])
+    for e, s, v in last:
+        Q[e].wait_ge(T.sem[s], v)

import math
from concourse.bass import DstId, RemoteDMATransfer
from concourse.mybir import AluOpType as ALU, ActivationFunctionType as ACT

N, M, D = 8, 1024, 4
P = N * M
UP = 1 << 15
KEEP = UP * 2 * P + UP + 2 * P - 2
CFG = {"blocks": [[256, 256, 256, 256]] * 4,
       "ways": [["DDDDDDD"] * 4, ["DDDHDDD", "DDDHDDD", "PPPHHDD", "PPPHHDD"], ["DDDHDDD", "DDDHDDD", "PPPHHHD", "PPPHHHD"],
                ["PDDHDDD", "PDDHDDD", "PPPHHHD", "PPPHHHD"]],
       "lots": [[]] + [[[0, 1], [2, 3]]] * 3, "heng": ["G", "VSG", "VSG", "VSG"], "twice": ["P"] * 3,
       "turns": [[4, 5], [6, 7], [2, 3], [1]], "stores": [[0, 1], [2], [3]], "frow": 0.038, "look": [256, 512, 512, 512], "hold": True,
       "lead": [[("S", 0, 128), ("V", 128, 256)], [("S", 0, 256)], [("S", 0, 512)], []],
       "fill": [[("G", 1024), ("S", 512), ("S", 512), ("V", 2048)], [("S", 512), ("S", 512), ("S", 512), ("V", P)]],
       "pairs": [[0], [1], [2, 3]], "small": "VS", "heads": [[], [1]], "aff": "VS",
       "order": ["ld", "seed", "tr", "xr", "own", "tf0", "on", "tb0", "tb1", "remote", "o1", "ab", "ae", "p1", "head00", "head10",
                 "head11", "a0", "l0", "r0", "a1", "a2", "s0", "l1", "r1", "s1", "l2", "r2", "s2", "s3"], "lag": 0.5,
       "early": {"su": 8.0}, "rounds": 30000, "heat": 0.006, "seed": 2,
       "paces": [(1.0, 1.0, 1.0, 1.0, 0.7, 1.6, 53.0), (1.0, 1.0, 1.0, 0.9, 1.6, 2.0, 53.0), (1.38, 1.12, 1.1, 1.1, 1.0, 1.8, 64.0),
                 (0.75, 0.88, 0.9, 1.1, 1.0, 1.7, 49.0)], "both": ["xr", "tb", "ow", "tr", "st"],
       "rate": 920e3, "row": 0.023, "td": 1.7, "tr": 1.6, "far": 20e3, "gat": 1.6, "pe": 0.48, "iss": 0.08}

SCRATCH = {"tr": ("dram", [D, P], "int32"), "dsrc": ("dram", [N, 128, 128], "float32"), "xin": ("dram", [N, 128, 128], "float32"),
           "xr": ("sbuf", [128, N, 128], "int32"), "xf": ("sbuf", [128, N, 128], "float32"),
           "xg": ("sbuf", [128, N, 128], "float32"), "ddst": ("dram", [N, 128, 128], "float32"),
           "wa": ("sbuf", [128, P + 8], "float32"), "wb": ("sbuf", [128, P + 8], "float32")}
for _t, _l in (("int32", (("tb", P + 8), ("il", 192), ("i64", 4), ("jj", 4), ("pi", 256), ("y1", 256), ("q1", 256), ("n1", 256),
                          ("ia", D * 64), ("ib", D * 64), ("ic", D * 64), ("ci", D * 128))),
               ("uint16", (("off", D * 128), ("ls", D * 128), ("lo", 64))),
               ("float32", (("ones", 256), ("rot", 256), ("two", 256), ("kc", 4), ("ab", 512), ("ae", 512), ("tz", D * 64),
                            ("half", 128), ("sel", 128), ("rr", 2 * D * M), ("ga", M), ("gs", M), ("yo", M), ("yf", M)))):
    for _n, _c in _l:
        SCRATCH[_n] = ("sbuf", [128, _c], _t)
for _n in ("pw0", "pw1", "pr0", "pr1", "pc0", "pc1", "pc2", "pc3"):
    SCRATCH[_n] = ("psum", [128, 512], "float32")
SEMAPHORES = ["cV", "cS", "cP", "cG", "sent", "arr0", "arr1", "fa0", "fa1", "fa2", "fa3", "fa4", "fa5", "fa6"] + ["d%d" % _i for _i in range(48)]
KEPT = {}


def runs(first, count):
    first %= N
    head = min(count, N - first)
    return [(0, first, head)] + ([(head, 0, count - head)] if count > head else [])


def build(g, core, T, topo, rank):
    ops = []
    Q = {"V": g.vector, "S": g.scalar, "P": g.tensor, "G": g, "Y": g.sync}
    GAT, PE = CFG["gat"], CFG["pe"] * 1e-3
    nsem, stage = [0], ["head"]

    def node(tag, kind, engs, emit, rd, wr, sem=None, n=0, xfer=0.0, par=(), last=False):
        ops.append({"tag": tag, "kind": kind, "engs": engs, "cost": min(engs.values()) if engs else 0.0, "emit": emit,
                    "rd": list(rd), "wr": list(wr), "par": list(par), "sem": sem, "n": n, "xfer": xfer, "last": last,
                    "gat": tag[:2] in ("lk", "ga", "gs", "zo"),
                    "stage": (CFG["order"] + stage).index(tag if tag in CFG["order"] and stage[0] == "head" else stage[0])})

    def comp(tag, eng, cost, emit, rd, wr):
        node(tag, "c", {eng: cost}, lambda e: emit(), rd, wr)

    def copy(tag, out, in_, n, rd, wr, per=1.0, scale=None, engs="VS"):
        def emit(e):
            if e == "G":
                return [g.affine_select(out, in_, [[0, n]], ALU.is_ge, 0.0, 0, 0)]
            if e == "V":
                if scale is None:
                    return [g.vector.tensor_copy(out, in_)]
                return [g.vector.tensor_scalar(out, in_, scale, None, ALU.mult)]
            if scale is None:
                return [g.scalar.activation(out, in_, ACT.Copy)]
            return [g.scalar.activation(out, in_, ACT.Copy, scale=scale)]
        c = {"V": 0.06 + n * per * 1e-3, "S": 0.075 + n * per * 1e-3, "G": 0.32 + n * 2.08e-3}
        node(tag, "c", {e: c[e] for e in engs}, emit, rd, wr)

    def aff(tag, out, in_, scale, bias, n, rd, wr, floor=False):
        def emit(e):
            if e == "S":
                return [g.scalar.activation(out, in_, ACT.Relu if floor else ACT.Identity, bias=bias, scale=scale)]
            if floor:
                return [g.vector.tensor_scalar(out, in_, -bias / scale, scale, ALU.is_gt, ALU.mult)]
            return [g.vector.tensor_scalar(out, in_, scale, bias, ALU.mult, ALU.add)]
        node(tag, "c", {e: {"V": 0.06, "S": 0.075}[e] + n * 1e-3 for e in CFG["aff"]}, emit, rd, wr)

    def ts(tag, out, in0, s1, s2, op0, op1, n, rd, wr):
        more = [] if op1 is None else [op1]
        comp(tag, "V", 0.06 + n * 1e-3, lambda: [g.vector.tensor_scalar(out, in0, s1, s2, op0, *more)], rd, wr)

    def tt(tag, out, a, b, op, cyc, rd, wr):
        comp(tag, "V", 0.06 + cyc * 1e-3, lambda: [g.vector.tensor_tensor(out, a, b, op)], rd, wr)

    def fill(ap, val, cyc, wr, tag="fill"):
        comp(tag, "V", 0.06 + cyc * 1e-3, lambda: [g.vector.memset(ap, val)], [], wr)

    def pick(out, in_, pat, n, rd, wr):
        comp("pick", "G", 0.32 + n * 2.08e-3, lambda: [g.affine_select(out, in_, pat, ALU.is_equal, 0.0, 0, 1)], rd, wr)

    def mms(tag, items, cyc, rd, wr):
        comp(tag, "P", cyc * PE, lambda: [g.tensor.matmul(*x) for x in items][-1:], rd, wr)

    def dma(tag, pairs, rd, wr, nbytes, rows, par=(), last=False, eng="Y"):
        nsem[0] += 1
        node(tag, "d", {e: CFG["iss"] * len(pairs) for e in (eng if tag[:2] not in CFG["both"] else "YS")}, lambda e: [Q[e].dma_start(o, i) for o, i in pairs], rd, wr,
             sem="d%d" % (nsem[0] - 1), n=16 * len(pairs), xfer=nbytes / CFG["rate"] + rows * CFG["row"] / 16, par=par,
             last=last)

    def remote(items, sem, rd, tok, nbytes):
        ne = min(len(topo.engines(core, T.cores[r])) for _s, _d, r in items)
        w = 1
        while 2 * w * len(items) <= ne:
            w *= 2

        def emit(_e):
            trs = []
            for k, (src, dst, r) in enumerate(items):
                mask = sum(1 << x for x in topo.engines(core, T.cores[r])[k * w:(k + 1) * w])
                rid, pid = topo.addr(T.cores[r], core)
                trs.append(RemoteDMATransfer(dst_ids=[DstId(rid=rid, pnc=pid)], dma_engine_mask=mask,
                                             remote_sem=T.sem[sem], src=src, dst=dst))
            g.remote_dma_fused(trs, local_sem=T.sem.sent)
            return []
        node("remote", "r", {"G": 0.4}, emit, rd, [tok, "ring"], sem="sent", n=w * len(items), xfer=nbytes / w / CFG["far"])
        return w * len(items)

    W = [T.wa, T.wb]
    SH, AND = ALU.logical_shift_right, ALU.bitwise_and

    def wtok(b, k, c0, c1, halves=(0, 1)):
        return [("w", b, k, q, h) for q in range(c0 // 128, c1 // 128) for h in halves]

    def part(b, k, c0, c1, p0=0, p1=128):
        return W[b][p0:p1, M * k + c0:M * k + c1]

    def wall(b):
        return [t for k in range(N) for t in wtok(b, k, 0, M)] + [("wz", b)]

    waves = [range(1, 5), range(5, 8)]
    for s, ts_ in enumerate(waves):
        dma("ld", [(T.dsrc[ts_[0] + o:ts_[0] + o + n], T.v[16 * r:16 * (r + n), :]) for o, r, n in runs(rank + ts_[0], len(ts_))],
            [], [("dsrc", s)], 65536 * len(ts_), 16)
    dma("tr", [(T.tr[:], T.tree[rank:rank + 1, :])], [], ["tr"], 131072, 16)
    c, seed, tbs = 0, P - 512, []
    fill(T.tb[:, seed:P], 0, 512, [("tf", seed)], "seed")
    for h, pieces in enumerate(CFG["fill"]):
        c0, tag = c, "tf%d" % h
        for e, n in pieces:
            n, tok = min(n, seed - c), [("tf", c)]
            if e == "V":
                fill(T.tb[:, c:c + n], 0, n, tok, tag)
            elif e == "S":
                copy(tag, T.tb[:, c:c + n], T.tb[:, seed:seed + n], n, [("tf", seed)], tok, engs="S")
            else:
                comp(tag, "G", 0.15 + n * 2e-3, lambda c=c, n=n: [g.iota(T.tb[:, c:c + n], [[1, n]], 0, 0)], [], tok)
            c += n
        more = [("tf", seed)] + [t for x in tbs for t in x[2]] if c == seed else []
        tbs.append((c0, P if more else c, [o["wr"][0] for o in ops[-len(pieces):]] + more))
    fill(T.tb[:, P:P + 8], 2 * P, 64, ["tbz"])
    for h in range(4):
        dma("xr", [(T.xr[8 * d:8 * d + 8, q, :], T.tree[rank:rank + 1, P * d + M * q:P * d + M * q + M])
                   for d in range(D - 1) for q in range(2 * h, 2 * h + 2)]
            + [(T.xr[8 * D - 8:8 * D, :, :], T.tree[rank:rank + 1, P * (D - 1):P * D])][h:], [], [("xr", h)], 32768, 64)
    xr = [("xr", h) for h in range(4)]
    for h, (c0, c1, toks) in enumerate(tbs):
        for u in range(2):
            dma("tb%d" % h, [(T.tb[16 * s:16 * s + D, c0:c1], T.tr[:, c0:c1]) for s in range(4 * u, 4 * u + 4)], ["tr"] + toks, [],
                64 * (c1 - c0), 16, par=["tb"])
    comp("lo", "G", 0.4, lambda: [g.iota(T.il[:, 0:64], [[M, N], [16, N]], P, 1)], tbs[-1][2] if CFG["hold"] else [], ["il0"])
    for s, ts_ in enumerate(waves):
        got = remote([(T.dsrc[t], T.xin[N - t], (rank + t) % N) for t in ts_], "arr%d" % s,
                     [("dsrc", s)] + (["il0"] if s and CFG["hold"] else []), ("s", s), 65536)
        node("arr", "x", {}, None, [("s", s)], [("xin", s)], sem="arr%d" % s, n=got)

    def slots(tag, src, rel, count, ks, rd):
        pairs = [(part(0, k, 0, M, 16 * j, 16 * (j + n)), src(rel + o, n))
                 for k in ks for o, j, n in runs(rank + rel - k, count)]
        dma(tag, pairs, rd, [], 65536 * count * len(ks), 16 * count * len(ks), par=[t for k in ks for t in wtok(0, k, 0, M)])
    byd = [0] + [k for k in range(1, N) if CFG["ways"][0][0][k - 1] == "D"]
    slots("own", lambda r, n: T.v[16 * rank:16 * rank + 16, :], 0, 1, byd, [])
    for s, ts_ in enumerate(waves):
        cut = [0] + CFG["heads"][s] + [N]
        for i in range(len(cut) - 1):
            slots("head%d%d" % (s, i), lambda r, n: T.xin[r:r + n], N - ts_[-1], len(ts_), byd[cut[i]:cut[i + 1]], [("xin", s)])

    fill(T.ones[:, :], 1.0, 256, ["ones"], "on")
    fill(T.half[:, 0:128], 0.5, 128, ["half"])
    fill(T.half[:, 64:128:2], UP / 2, 64, ["half"])
    pick(T.rot[:, :], T.ones[:, :], [[0, 2], [-1, 128]], 256, ["ones"], ["rot"])
    for lv in range(2):
        pick(T.sel[:, 64 * lv:64 * lv + 64], T.half[:, 64 * lv:64 * lv + 64], [[-1, D], [-16, N], [0, 2]], 64, ["half"], ["sel"])
    comp("i64", "G", 0.15, lambda: [g.iota(T.i64[:, :], [[16, 4]], 0, 1)], [], ["i64"])
    ts("jj", T.jj[:, 0:1], T.i64[:, 0:1], 4, None, ALU.arith_shift_right, None, 64, ["i64"], ["jj"])
    ts("kc", T.kc[:, 0:1], T.jj[:, 0:1], -float(M), float(P), ALU.mult, ALU.add, 64, ["jj"], ["kc"])
    ts("kc2", T.kc[:, 1:2], T.jj[:, 0:1], -2.0 * M, 2.0 * P, ALU.mult, ALU.add, 64, ["jj"], ["kc2"])
    aff("ab1", T.ab[:, 1:512:2], T.ones[:, :], 0.0, -0.25, 256, ["ones"], ["ab1"])
    aff("ae1", T.ae[:, 1:512:2], T.ones[:, :], 0.0, T.kc[:, 0:1], 256, ["ones", "kc"], ["ae1"])
    copy("two", T.two[:, 0:128], T.rot[:, 0:128], 128, ["rot"], ["two"], scale=2.0)
    copy("six", T.two[:, 128:256], T.rot[:, 0:128], 128, ["rot"], ["six"], scale=0.5 ** D)
    ts("kc3", T.kc[:, 2:3], T.jj[:, 0:1], 128.0 - 16.0 - M, None, ALU.mult, None, 64, ["jj"], ["kc3"])
    ts("lo", T.il[:, 64:128], T.il[:, 0:64], T.kc[:, 2:3], None, ALU.add, None, 64, ["il0", "kc3"], ["il1"])
    ts("lo", T.il[:, 128:192], T.il[:, 64:128], P - 1, None, AND, None, 64, ["il1"], ["il2"])
    copy("lo", T.lo[:, :], T.il[:, 128:192], 64, ["il2"], ["lo"], engs="V")
    fill(T.wa[:, P:P + 8], 0.0, 64, [("wz", 0)])
    fill(T.wb[:, P:P + 8], 0.0, 64, [("wz", 1)])

    for h in range(2):
        copy("xf", T.xf[0:32, 4 * h:4 * h + 4, :], T.xr[0:32, 4 * h:4 * h + 4, :], 512, xr, [("xf", h)])
    for i in range(N):
        copy("xg", T.xg[0:32, i, :], T.xr[0:32, :, 16 * i:16 * i + 16], 128, xr, [("xg", i)])
    cf, cb, eye = T.pw0, T.pw1, T.rot[0:32, 0:32]
    for h in range(2):
        mms("cf", [(cf[:, i:256:8], T.xg[0:32, i, :], eye, True, True) for i in range(4 * h, 4 * h + 4)], 1024,
            [("xg", i) for i in range(4 * h, 4 * h + 4)] + ["rot"], [("pw", 0)])
    for h in range(2):
        mms("cb", [(cb[:, q:256:8], T.xf[0:32, q, :], eye, True, True) for q in range(4 * h, 4 * h + 4)], 1024,
            [("xf", h), "rot"], [("pw", 1)])
    ts("pi", T.pi[:, :], cf[:, 0:256], 0.5, -0.25, ALU.mult, ALU.add, 256, [], [("pw", 0), "pi"])
    copy("o1", T.off[:, 0:256], T.pi[:, :], 256, ["pi"], ["o1"], engs="V")
    copy("ab", T.ab[:, 0:512:2], cb[:, 0:256], 256, [], [("pw", 1), "ab0"], scale=-0.5)
    aff("y1", T.y1[:, :], cf[:, 0:256], 1.0, T.kc[:, 1:2], 256, ["kc2"], [("pw", 0), "y1"])
    aff("n1", T.n1[:, :], cf[:, 0:256], float(P), -float(P) * (2 * P - 1), 256, [], [("pw", 0), "n1"], floor=True)
    ts("sf", T.q1[:, :], T.y1[:, :], 1, None, AND, None, 256, ["y1"], ["q1"])
    aff("ae", T.ae[:, 0:512:2], T.q1[:, :], UP / 2, -UP / 2, 256, ["q1"], ["ae0"])
    ts("p1", T.y1[:, :], T.y1[:, :], 1, P - 1, SH, AND, 256, ["q1"], ["y1"])
    tt("p1", T.pi[:, :], T.y1[:, :], T.n1[:, :], ALU.max, 512, ["y1", "n1"], ["pi"])
    ts("p1", T.ls[:, 0:256], T.pi[:, :], float(P), None, ALU.min, None, 256, ["pi"], ["l1"])

    PC = [T.pc0, T.pc1, T.pc2, T.pc3]

    def look(ds, lv, bk, first, rd, rd2):
        pc, n = PC[bk], 128 * len(ds)
        mms("dl", [(pc[:, 256 * lv:256 * lv + n], T.rot[:, 0:128], first[:, 128 * ds[0]:128 * ds[0] + n], True, False)], 4 * n,
            ["rot"] + rd2, [("pc", bk)])
        for d in ds:
            c0, o0, col, s0 = M * (2 * d + lv), 256 * lv + 64 * d, 256 * lv + 128 * (d - ds[0]), 64 * lv + 16 * d
            n = CFG["look"][d]
            for h in range(M // n):
                copy("lk%d%d" % (d, lv), T.rr[:, c0 + n * h:c0 + n * h + n],
                     T.tb[:, 0:P + 8].indirect(T.off[:, o0 + n // 16 * h:o0 + n // 16 * (h + 1)]), n, ["tb", "tbz"] + rd,
                     [("r", d, lv, h)], per=GAT)
                mms("dl%d%d" % (d, lv),
                    [(pc[:, col + 16 * a:col + 16 * a + 16], T.rr[:, c0 + 128 * a:c0 + 128 * a + 128], T.sel[:, s0:s0 + 16],
                      False, a == N - 1 and d == ds[-1]) for a in range(n // 128 * h, n // 128 * (h + 1))],
                    2 * n, ["sel", ("r", d, lv, h)], [("pc", bk)])

    def lists(i, ds):
        d, n = ds[0], 64 * len(ds)
        x, bk = slice(64 * d, 64 * d + n), ("pc", i)
        even, odd = PC[i][:, 0:2 * n:2], PC[i][:, 1:2 * n:2]
        look(ds, 0, i, T.ab, ["o1"], ["ab0", "ab1"])
        copy("z1", T.ia[:, x], even, n, [], [bk, ("ia", d)], scale=2.0, engs=CFG["small"])
        ts("z2", T.ib[:, x], T.ia[:, x], 1, None, AND, None, n, [("ia", d)], [("ib", d)])
        tt("z3", T.tz[:, x], T.ib[:, x], even, ALU.mult, n, [("ib", d)], [bk, ("tz", d)])
        tt("z4", T.ic[:, x], odd, T.tz[:, x], ALU.subtract, n, [("tz", d)], [bk, ("ic", d)])
        copy("z5", T.off[:, 256 + 64 * d:256 + 64 * d + n], T.ic[:, x], n, [("ic", d)], [("o2", d)], engs="V")
        stage[0] = "l%d" % d
        look(ds, 1, i, T.ae, [("o2", d)], ["ae0", "ae1"])
        c0, c1 = 128 * d, 128 * d + 2 * n
        copy("f1", T.ci[:, c0:c1], PC[i][:, 256:256 + 2 * n], 2 * n, [], [bk, ("ci", d)], scale=2.0, engs=CFG["small"])
        ts("f2", T.ci[:, c0:c1], T.ci[:, c0:c1], KEEP, None, AND, None, 2 * n, [], [("ci", d)])
        tt("f3", T.ic[:, x], T.ci[:, c0:c1:2], T.ci[:, c0 + 1:c1:2], ALU.max, 2 * n, [("ci", d)], [("ic", d)])
        ts("ls%d" % d, T.ls[:, 256 + 64 * d:256 + 64 * d + n], T.ic[:, x], 0.5, float(P), ALU.mult, ALU.min, n, [("ic", d)],
           [("l2", e) for e in ds])

    nb = [0]

    def bank(d):
        pool = [(T.pr0, ("pr", 0)), (T.pr1, ("pr", 1))] + [(PC[i], ("pc", i)) for i in range(D) if max((CFG["pairs"] + [[-1]] * D)[i]) < d]
        nb[0] += 1
        return pool[nb[0] % len(pool)]

    def edges(d):
        out = [0]
        for n in CFG["blocks"][d]:
            out.append(out[-1] + n)
        return out

    def spread(d):
        b, e = d % 2, edges(d - 1)
        ways = CFG["ways"][d]
        for lot in CFG["lots"][d]:
            pairs, rd, wr, count = [], [], [], 0
            for k in range(1, N):
                cs = [t for t in lot if ways[t][k - 1] == "D"]
                if cs:
                    c0, c1, s = e[cs[0]], e[cs[-1] + 1], 16 * k
                    pairs.append((part(b, k, c0, c1, 0, 128 - s), part(b, 0, c0, c1, s, 128)))
                    pairs.append((part(b, k, c0, c1, 128 - s, 128), part(b, 0, c0, c1, 0, s)))
                    rd += wtok(b, 0, c0, c1)
                    wr += wtok(b, k, c0, c1)
                    count += c1 - c0
            if pairs:
                dma("rep%d" % d, pairs, sorted(set(rd)), wr, 512 * count, 64 * len(pairs))
        for t in range(len(ways)):
            c0, c1 = e[t], e[t + 1]
            n = c1 - c0
            for k in range(1, N):
                if ways[t][k - 1] == "P":
                    pr, bk = bank(d)
                    mms("rot", [(pr[:, 0:n], T.rot[:, 16 * k:16 * k + 128], part(b, 0, c0, c1), True, True)], 4 * n,
                        ["rot"] + wtok(b, 0, c0, c1), [bk])
                    copy("pc", part(b, k, c0, c1), pr[:, 0:n], n, [], [bk] + wtok(b, k, c0, c1))
                if ways[t][k - 1] == "H":
                    for h in range(2):
                        copy("hc", part(b, k, c0, c1, 64 * h, 64 * h + 64), part(b, k - 4, c0, c1, 64 - 64 * h, 128 - 64 * h), n,
                             wtok(b, k - 4, c0, c1, (1 - h,)), wtok(b, k, c0, c1, (h,)), engs=CFG["heng"][d])

    PW = [T.pw0, T.pw1]

    def step(d, c0, c1, lead):
        b, n = d % 2, c1 - c0
        blks = range(c0 // 128, c1 // 128)
        win = W[b][:, 0:P + 8]
        o1, o2 = 64 * d + c0 // 16, 256 + 64 * d + c0 // 16
        for e, x0, x1 in lead:
            copy("ga%d" % d, T.ga[:, c0 + x0:c0 + x1], win.indirect(T.ls[:, o2 + x0 // 16:o2 + x1 // 16]), x1 - x0,
                 wall(b) + [("l2", d)], [("ga", q) for q in range((c0 + x0) // 128, (c0 + x1) // 128)], per=GAT, engs=e)
        tt("gs", T.gs[:, c0:c1], win.indirect(T.ls[:, o1:o1 + n // 16]), T.ga[:, c0:c1], ALU.add, GAT * n,
           wall(b) + ["l1"] + [("ga", q) for q in blks], [("gs", q) for q in blks])
        if d < D - 1:
            tt("su%d" % d, part(1 - b, 0, c0, c1), PW[c0 // 512][:, c0 % 512:c0 % 512 + n], T.gs[:, c0:c1], ALU.subtract, n,
               [("gs", q) for q in blks], wtok(1 - b, 0, c0, c1) + [("pw", c0 // 512)])
            return
        pr, bk = bank(d)
        copy("zo", T.yo[:, c0:c1], win.indirect(T.lo[:, c0 // 16:c1 // 16]), n, wall(b) + ["lo"], [("yo", q) for q in blks],
             per=GAT, scale=0.5 ** d)
        mms("hv", [(pr[:, 0:n], T.two[:, 128:256], T.gs[:, c0:c1], True, True)], 4 * n, ["six"] + [("gs", q) for q in blks], [bk])
        tt("su%d" % d, T.yf[:, c0:c1], T.yo[:, c0:c1], pr[:, 0:n], ALU.subtract, n, [("yo", q) for q in blks],
           [bk] + [("yf", q) for q in blks])

    for i, ds in enumerate(CFG["pairs"]):
        stage[0] = "a%d" % ds[0]
        lists(i, ds)
    for d in range(D - 1):
        stage[0] = "r%d" % d
        spread(d)
        stage[0] = "s%d" % d
        for h in range(2):
            src, rd = part(d % 2, 0, 512 * h, 512 * h + 512), wtok(d % 2, 0, 512 * h, 512 * h + 512)
            if CFG["twice"][d] == "P":
                mms("tw", [(PW[h][:, :], T.two[:, 0:128], src, True, True)], 2048, rd + ["two"], [("pw", h)])
            else:
                copy("tw", PW[h][:, :], src, 512, rd, [("pw", h)], scale=2.0)
        e = edges(d)
        for t in range(len(e) - 1):
            step(d, e[t], e[t + 1], CFG["lead"][t])

    stage[0] = "r%d" % (D - 1)
    spread(D - 1)
    stage[0] = "s%d" % (D - 1)
    turns = [sorted(rank ^ x for x in xs) for xs in CFG["turns"]] + [[rank]]
    nt = len(turns) - 1
    for t, qs in enumerate(turns):
        step(D - 1, 128 * qs[0], 128 * qs[-1] + 128, [("S", 0, 128 * len(qs))])
        if t < nt:
            got = remote([(T.yf[:, 128 * q:128 * q + 128], T.ddst[rank], q) for q in qs], "fa%d" % t,
                         [("yf", q) for q in qs], ("f", t), 128 * CFG["frow"] * CFG["far"])
            node("arr", "x", {}, None, [("f", t)], [("dd", t)], sem="fa%d" % t, n=got)
    for lot in [[nt]] + CFG["stores"]:
        a, z = min(turns[t][0] for t in lot), max(turns[t][-1] for t in lot) + 1
        for e, js in (("Y", range(0, 4)), ("S", range(4, 8))):
            if lot[0] < nt:
                src, rd = [T.ddst[a:z, 16 * j:16 * j + 16, :] for j in js], [("dd", t) for t in lot]
            else:
                src, rd = [T.yf[16 * j:16 * j + 16, 128 * a:128 * z] for j in js], [("yf", a)]
            dma("st", [(T.y[16 * a:16 * z, 128 * j:128 * j + 128], s) for j, s in zip(js, src)], rd, [], 32768 * (z - a),
                64 * (z - a), last=True, eng=e)
    return ops, Q


def plan(ops):
    n = len(ops)
    deps, soft = [set() for _ in range(n)], [set() for _ in range(n)]
    writer, readers = {}, {}
    for i, o in enumerate(ops):
        for t in o["rd"] + o["wr"]:
            deps[i].update(writer.get(t, ()))
        for t in o["wr"] + o["par"]:
            deps[i].update(readers.get(t, ()))
        for t in o["rd"]:
            readers.setdefault(t, []).append(i)
        for t in o["wr"]:
            writer[t] = [i]
            readers[t] = []
        for t in o["par"]:
            writer.setdefault(t, []).append(i)
        deps[i].discard(i)
        soft[i] = {j for j in deps[i] if o["kind"] == "r" and ops[j]["kind"] == "r"}
        deps[i] -= soft[i]
    tail = {"c": 0.1, "d": CFG["td"], "r": CFG["tr"], "x": 0.0}
    succ = [[] for _ in range(n)]
    for i in range(n):
        for j in sorted(deps[i] | soft[i]):
            succ[j].append(i)
    prio = [0.0] * n
    for i in range(n - 1, -1, -1):
        prio[i] = ops[i]["cost"] + ops[i]["xfer"] + max(
            [prio[k] + (0.0 if i in soft[k] else tail[ops[i]["kind"]]) for k in succ[i]] + [tail[ops[i]["kind"]]])
    stage = [o["stage"] for o in ops]
    for i in range(n - 1, -1, -1):
        stage[i] = min([stage[i]] + [stage[k] for k in succ[i]])
        prio[i] += CFG["early"].get(ops[i]["tag"][:2], 0.0)
        prio[i] = max([prio[i]] + [prio[k] + 1e-6 for k in succ[i] if stage[k] == stage[i]])

    def gap(busy, t, c):
        for a, z in busy:
            if a - t >= c - 1e-9:
                break
            t = max(t, z)
        return t

    busy = {e: [] for e in "VSPGYdr"}
    end, qend, start, eng = [0.0] * n, [0.0] * n, [0.0] * n, [None] * n
    for i in sorted(range(n), key=lambda i: (stage[i], -prio[i], i)):
        o, k = ops[i], ops[i]["kind"]
        t0 = max([end[j] for j in deps[i]] + [qend[j] for j in soft[i]] + [0.0])
        if k == "x":
            start[i] = end[i] = t0
            continue
        while True:
            t, e = min((gap(busy[x], t0, c) + c, x) for x, c in o["engs"].items())
            t1 = t - o["engs"][e] + CFG["iss"]
            if k != "d" or gap(busy[k], t1, o["xfer"]) <= t1 + CFG["lag"] + 1e-6:
                break
            t0 = gap(busy[k], t1, o["xfer"]) - CFG["iss"] - CFG["lag"]
        start[i], qend[i], eng[i] = t - o["engs"][e], t, e
        busy[e] = sorted(busy[e] + [(start[i], t)])
        if k != "c":
            t1 = gap(busy["d"], start[i] + CFG["iss"] if k == "d" else t, o["xfer"])
            busy["d"] = sorted(busy["d"] + [(t1, t1 + o["xfer"])])
            t = max(t, t1 + o["xfer"])
        end[i] = t + tail[k]
    before = [deps[i] | soft[i] for i in range(n)]
    if "order" not in KEPT:
        KEPT["order"], KEPT["eng"] = polish(ops, sorted(range(n), key=lambda i: (start[i], i)), eng, deps, before)
    todo, order, placed = list(KEPT["order"]), [], set()
    while todo:
        i = next(x for x in todo if before[x] <= placed)
        todo.remove(i)
        placed.add(i)
        order.append((i, KEPT["eng"][i], start[i]))
    return order, deps, end


def polish(ops, order, eng, deps, before):
    n = len(ops)
    kind, pe = [o["kind"] for o in ops], ["P" in o["engs"] for o in ops]
    paces = []
    for gat, vec, ten, ring, iss, td, unit in CFG["paces"]:
        f = [iss if o["kind"] == "d" else 1.0 if o["kind"] != "c" else ten if "P" in o["engs"] else gat if o["gat"] else vec
             for o in ops]
        paces.append(([{e: c * f[i] for e, c in o["engs"].items()} for i, o in enumerate(ops)], [o["xfer"] * ring for o in ops],
                      {"c": 0.1, "d": td, "r": CFG["tr"], "i": iss * CFG["iss"]}, unit))

    def run(order, eng, pace):
        cost, xfer, tail, unit = pace
        free, last = dict.fromkeys("VSPGYdr", 0.0), {}
        end, by = [0.0] * n, [(-1, False)] * n
        for i in order:
            e, k, t, b = eng[i], kind[i], 0.0, (-1, False)
            for j in deps[i]:
                x = end[j] - 0.1 if pe[i] and pe[j] else end[j]
                if x > t:
                    t, b = x, (j, False)
            if e is not None:
                if free[e] > t:
                    t, b = free[e], (last[e], True)
                t0, t = t, t + cost[i][e]
                free[e], last[e] = t, i
                if k != "c":
                    t0 = t0 + tail["i"] if k == "d" else t
                    if free["d"] > t0:
                        t0, b = free["d"], (last["d"], True)
                    free["d"], last["d"] = t0 + xfer[i], i
                    t = max(t, free["d"])
                t += tail[k]
            end[i], by[i] = t, b
        i, chain = end.index(max(end)), []
        while i >= 0:
            chain.append((i,) + by[i])
            i = by[i][0]
        return (max(end) / unit) ** 4, chain

    seed = [CFG["seed"]]

    def rnd():
        seed[0] = (seed[0] * 1103515245 + 12345) % 2147483648
        return seed[0] / 2147483648.0

    now = [run(order, eng, p) for p in paces]
    best = (sum(r[0] for r in now), order, eng)
    for it in range(CFG["rounds"]):
        chain = now[int(rnd() * len(now))][1]
        i, j, queued = chain[int(rnd() * len(chain))]
        new, e2, r = order, eng, rnd()
        if r < 0.3:
            x = i if r < 0.15 or j < 0 else j
            other = [y for y in ops[x]["engs"] if y != eng[x]]
            if not other:
                continue
            e2 = list(eng)
            e2[x] = other[int(rnd() * len(other))]
        else:
            if r < 0.4:
                i = int(rnd() * n)
                j = next((x for x in reversed(order[:order.index(i)]) if eng[x] == eng[i]), -1)
                queued = j >= 0 and eng[i] is not None
            if not queued:
                continue
            p, q = order.index(i), order.index(j)
            span, need = order[q:p + 1], {i}
            for x in reversed(span):
                if x in need:
                    need |= before[x]
            if j in need:
                continue
            new = order[:q] + [x for x in span if x in need] + [x for x in span if x not in need] + order[p + 1:]
        then = [run(new, e2, p) for p in paces]
        worse = sum(r[0] for r in then) - sum(r[0] for r in now)
        if worse <= 0 or rnd() < math.exp(-worse / (CFG["heat"] * (1.001 - it / CFG["rounds"]))):
            order, eng, now = new, e2, then
            if sum(r[0] for r in now) < best[0]:
                best = (sum(r[0] for r in now), order, eng)
    return best[1], best[2]


def rank_program(g, core, T, topo):
    rank = T.rank_of(core)
    if rank is None:
        return
    ops, Q = build(g, core, T, topo, rank)
    order, deps, _end = plan(ops)
    count = {e: 0 for e in "VSPG"}
    done, total, waited, last = {}, {"sent": 0}, {}, []
    seen = {e: {} for e in "VSPGY"}
    for i, e, _t in order:
        o = ops[i]
        if o["kind"] == "x":
            done[i] = (o["sem"], o["n"])
            total[o["sem"]] = o["n"]
            continue
        need = {"cG": count["G"]} if e == "G" and o["kind"] == "c" else {}
        for j in deps[i]:
            s, v = done[j]
            if not (s == "cP" and e == "P"):
                need[s] = max(need.get(s, 0), v)
        for s in sorted(need):
            if need[s] > seen[e].get(s, 0):
                Q[e].wait_ge(T.sem[s], need[s])
                seen[e][s] = need[s]
                waited[s] = max(waited.get(s, 0), need[s])
        ins = o["emit"](e)
        if o["kind"] == "c":
            for x in ins:
                x.then_inc(T.sem["c" + e], 1)
            count[e] += len(ins)
            done[i] = ("c" + e, count[e])
        elif o["kind"] == "d":
            for x in ins:
                x.then_inc(T.sem[o["sem"]], 16)
            done[i] = (o["sem"], o["n"])
            if o["last"]:
                last.append((e, o["sem"], o["n"]))
            else:
                total[o["sem"]] = o["n"]
        else:
            total["sent"] += o["n"]
    for e in "VSPG":
        total["c" + e] = count[e]
    for s in sorted(total):
        if total[s] > waited.get(s, 0):
            g.wait_ge(T.sem[s], total[s])
    for e, s, v in last:
        Q[e].wait_ge(T.sem[s], v)
